import numpy as np
import ml_dtypes


def mxq(x, axis, fmt="e4m3"):
    dtype, down = {"e4m3": (ml_dtypes.float8_e4m3fn, 7), "e5m2": (ml_dtypes.float8_e5m2, 14)}[fmt]
    v = np.moveaxis(np.asarray(x, np.float32).astype(ml_dtypes.bfloat16).astype(np.float64), axis, -1)
    blocks = v.reshape(v.shape[:-1] + (-1, 32))
    amax = np.abs(blocks).max(-1, keepdims=True)
    byte = np.maximum(np.where(amax > 0, np.frexp(amax)[1] - 1 + 127, 0) - down, 1)
    scale = np.exp2(byte - 127.0)
    codes = (blocks / scale).astype(np.float32).astype(dtype).astype(np.float64)
    return np.moveaxis((codes * scale).reshape(v.shape), -1, axis)


WIDE = False


def mx_kscale(k):
    if not WIDE:
        return np.ones(k)
    levels = np.array([10, -10, 5, -5, 0])
    if k % 512:
        return np.exp2(np.random.permutation(np.resize(levels, k // 32))).repeat(32)
    a = np.empty((k // 512, 16))
    for p in range(k // 512):
        a[p, :8] = np.random.permutation(np.resize(levels, 8))
        for g in range(8):
            far = levels[np.abs(levels - a[p, g]) >= 10]
            a[p, g + 8] = far[np.random.randint(len(far))]
    return np.exp2(a.ravel()).repeat(32)


def f64(x):
    return np.asarray(x).astype(np.float64)


def striped(idx):
    return np.tile(idx.reshape(-1, 16).T, (8, 1)).astype(np.uint16)


def unstriped(offs):
    return offs[:16].T.reshape(-1).astype(np.int64)


E2M1 = np.array([0.0, 0.5, 1.0, 1.5, 2.0, 3.0, 4.0, 6.0, -0.0, -0.5, -1.0, -1.5, -2.0, -3.0, -4.0, -6.0])


def pack_fp4(w):
    k, n = w.shape
    w = f64(np.asarray(w, np.float32).astype(ml_dtypes.bfloat16)).reshape(k // 32, 32, n)
    amax = np.abs(w).max(1)
    mant, ex = np.frexp(amax / 6.0)
    byte = np.clip(np.where(amax > 0, np.where(mant > 0.5, ex, ex - 1) + 127, 1), 1, 254)
    scaled = (w * np.exp2(127.0 - byte)[:, None, :]).reshape(k, n).astype(np.float32)
    c = np.ascontiguousarray(scaled.reshape(k // 512, 128, 4, n).transpose(0, 1, 3, 2)).astype(ml_dtypes.float4_e2m1fn).view(np.uint8) & 0xF
    words = (c[..., 0::2] | (c[..., 1::2] << 4)).reshape(k // 512, 128, 2 * n)
    return np.ascontiguousarray(words), np.ascontiguousarray(byte.astype(np.uint8).reshape(k // 512, 16, n))


def unpack_fp4(words, scales):
    g, _, n = scales.shape
    words = np.ascontiguousarray(words).reshape(g, 128, n, 2)
    nib = np.empty((g, 128, n, 4), np.uint8)
    nib[..., 0::2] = words & 0xF
    nib[..., 1::2] = words >> 4
    vals = E2M1[nib] * np.repeat(np.exp2(scales.astype(np.float64) - 127.0), 8, axis=1)[..., None]
    return vals.transpose(0, 1, 3, 2).reshape(g * 512, n)


def gelu(v):
    return 0.5 * v * (1.0 + np.tanh(np.sqrt(2.0 / np.pi) * (v + 0.044715 * v**3)))


K, T, S, V, N = 1024, 2048, 1024, 512, 128


def setup_inputs():
    n = np.random.standard_normal
    s = mx_kscale(K)[:, None]
    packed_xT = pack_fp4(n((K, T)) * s)
    return {
        "x_words": packed_xT[0],
        "x_scales": packed_xT[1],
        "w1": (n((K, N)) / np.sqrt(K) / s).astype(np.float32),
        "offs": striped(np.random.permutation(T)[:S]),
        "pos1": striped(np.random.permutation(S)[:V]),
        "pos2": striped(np.random.permutation(S)[:V]),
        "pos3": striped(np.random.permutation(S)[:V]),
    }


def reference(x_words, x_scales, w1, offs, pos1, pos2, pos3):
    xq = unpack_fp4(x_words, x_scales)[:, unstriped(offs)]
    y = gelu(mxq(f64(w1), 0, "e4m3").T @ xq)
    n0 = y[:, unstriped(pos1)]
    n1 = y[:, unstriped(pos2)]
    n2 = y[:, unstriped(pos3)]
    return np.maximum(np.minimum(n0, n1), np.minimum(np.maximum(n0, n1), n2))

@@ -1,0 +1,138 @@
+from contextlib import ExitStack
+
+import concourse.mybir as mybir
+
+K, T, S, V, M = 1024, 2048, 1024, 512, 128
+FLOPS = 2 * K * M * S
+
+F32 = mybir.dt.float32
+BF16 = mybir.dt.bfloat16
+I32 = mybir.dt.int32
+U32 = mybir.dt.uint32
+U16 = mybir.dt.uint16
+U8 = mybir.dt.uint8
+FP8X4 = mybir.dt.float8_e4m3fn_x4
+FP4X4 = mybir.dt.float4_e2m1fn_x4
+MAX = mybir.AluOpType.max
+MIN = mybir.AluOpType.min
+GELU = mybir.ActivationFunctionType.Gelu_apprx_tanh
+
+P = 128
+PACK = 4
+PASSES = K // (P * PACK)
+ROWS = 16
+GROUP = 128
+PIECES = ((512, 512), (384, 384, 256))
+HALF = V // 2
+
+
+def tile_picked_median_gelu_p_kernel(
+    tc, x_words, x_scales, w1, offs, pos1, pos2, pos3, out
+):
+    nc = tc.nc
+    with ExitStack() as ctx:
+        keep = ctx.enter_context(tc.tile_pool(name="keep", bufs=1))
+        psum = ctx.enter_context(tc.psum_pool(name="psum", bufs=1))
+
+        scale_table = keep.tile([P, T], U8, name="scale_table", align_bytes=64)
+        nc.sync.dma_start(
+            scale_table[0 : PASSES * ROWS, :].bitcast(I32),
+            x_scales.rearrange("z q c -> (z q) c").bitcast(I32),
+        )
+        offs_sb = keep.tile([P, S // 16], U16, name="offs_sb")
+        nc.sync.dma_start(offs_sb[:], offs)
+        nc.vector.memset(scale_table[32:64, :].bitcast(I32), 0)
+        nc.vector.memset(scale_table[64:128, :].bitcast(I32), 0)
+
+        word_table = [keep.tile([P, T], U16, name=f"word_table{z}", align_bytes=64) for z in range(PASSES)]
+        w_raw = keep.tile([P, PASSES, PACK, M], F32, name="w_raw")
+        nc.sync.dma_start(word_table[0][:].bitcast(I32), x_words[0].bitcast(I32))
+        nc.sync.dma_start(w_raw[:], w1.rearrange("(z p j) m -> p z j m", z=PASSES, j=PACK))
+        nc.sync.dma_start(word_table[1][:].bitcast(I32), x_words[1].bitcast(I32))
+        pos_sb = []
+        for d, pos in enumerate((pos1, pos2, pos3)):
+            pos_tile = keep.tile([P, V // 16], U16, name=f"pos_sb{d}")
+            nc.sync.dma_start(pos_tile[:], pos)
+            pos_sb.append(pos_tile)
+
+        x_plane = [keep.tile([P, S], U8, name=f"x_plane{z}", align_bytes=64) for z in range(PASSES)]
+        for z in range(PASSES):
+            nc.vector.memset(x_plane[z][:].bitcast(I32), 0)
+
+        picked_scales = keep.tile([P, S], U8, name="picked_scales", align_bytes=64)
+        nc.vector.tensor_copy(picked_scales[:], scale_table[:].indirect(offs_sb[:]))
+        for z in range(PASSES):
+            for q in range(4):
+                row = ROWS * z + 4 * q
+                nc.sync.dma_start(
+                    x_plane[z][32 * q : 32 * q + 4, :].bitcast(I32),
+                    picked_scales[row : row + 4, :].bitcast(I32),
+                )
+
+        def gather_words(z, first, width, tag):
+            codes = keep.tile([P, width], U16, name=f"x_codes{z}_{first}", tag=tag, align_bytes=64)
+            nc.vector.tensor_copy(
+                codes[:], word_table[z][:].indirect(offs_sb[:, first // 16 : (first + width) // 16])
+            )
+            return codes
+
+        banks = [psum.tile([M, GROUP], F32, name=f"bank{g}") for g in range(S // GROUP)]
+        y = keep.tile([P, S], F32, name="y")
+
+        codes0 = []
+        first = 0
+        for width in PIECES[0]:
+            codes0.append((first, width, gather_words(0, first, width, f"codes0_{first}")))
+            first = first + width
+
+        w_bf = keep.tile([P, PASSES, M, PACK], BF16, name="w_bf", tag="w_bf", align_bytes=64)
+        nc.scalar.copy(w_bf[:], w_raw[:].rearrange("p z j m -> p z m j"))
+        w_codes = keep.tile([P, PASSES * M], U32, name="w_codes", align_bytes=64)
+        w_plane = keep.tile([P, PASSES * M], U8, name="w_plane", align_bytes=64)
+        nc.vector.quantize_mx(
+            out=w_codes[:].bitcast(FP8X4), scales=w_plane[:], in_=w_bf[:].rearrange("p z m j -> p (z m j)")
+        )
+
+        def multiply(z, first, width, codes):
+            for c in range(0, width, GROUP):
+                g = (first + c) // GROUP
+                nc.tensor.matmul_mx(
+                    out=banks[g][:],
+                    lhsT=w_codes[:, z * M : (z + 1) * M].bitcast(FP8X4),
+                    lhsT_scale=w_plane[:, z * M : (z + 1) * M],
+                    rhs=codes[:, c : c + GROUP].bitcast(FP4X4),
+                    rhs_scale=x_plane[z][:, first + c : first + c + GROUP],
+                    start=(z == 0),
+                    stop=(z == PASSES - 1),
+                )
+                if z == PASSES - 1:
+                    nc.scalar.activation(y[:, g * GROUP : (g + 1) * GROUP], banks[g][:], GELU)
+
+        for first, width, codes in codes0:
+            multiply(0, first, width, codes)
+        first = 0
+        for width in PIECES[1]:
+            tag = "w_bf" if first == 0 else f"codes1_{first}"
+            multiply(1, first, width, gather_words(1, first, width, tag))
+            first = first + width
+
+        nb = []
+        for d in range(3):
+            fetched = keep.tile([P, V], F32, name=f"fetched{d}")
+            nc.vector.tensor_copy(fetched[:], y[:].indirect(pos_sb[d][:]))
+            nb.append(fetched)
+        hi = [keep.tile([P, HALF], F32, name=f"hi{h}") for h in range(2)]
+        lo = [keep.tile([P, HALF], F32, name=f"lo{h}") for h in range(2)]
+        cut = [keep.tile([P, HALF], F32, name=f"cut{h}") for h in range(2)]
+        med = [keep.tile([P, HALF], F32, name=f"med{h}") for h in range(2)]
+        cols = [slice(h * HALF, (h + 1) * HALF) for h in range(2)]
+        nc.vector.tensor_tensor(hi[0][:], nb[0][:, cols[0]], nb[1][:, cols[0]], MAX)
+        nc.vector.tensor_tensor(lo[0][:], nb[0][:, cols[0]], nb[1][:, cols[0]], MIN)
+        nc.vector.tensor_tensor(cut[0][:], hi[0][:], nb[2][:, cols[0]], MIN)
+        nc.vector.tensor_tensor(hi[1][:], nb[0][:, cols[1]], nb[1][:, cols[1]], MAX)
+        nc.vector.tensor_tensor(med[0][:], lo[0][:], cut[0][:], MAX)
+        nc.sync.dma_start(out[:, cols[0]], med[0][:])
+        nc.vector.tensor_tensor(cut[1][:], hi[1][:], nb[2][:, cols[1]], MIN)
+        nc.vector.tensor_tensor(lo[1][:], nb[0][:, cols[1]], nb[1][:, cols[1]], MIN)
+        nc.vector.tensor_tensor(med[1][:], lo[1][:], cut[1][:], MAX)
+        nc.sync.dma_start(out[:, cols[1]], med[1][:])

@@ -15,6 +15,8 @@ FP8X4 = mybir.dt.float8_e4m3fn_x4
 FP4X4 = mybir.dt.float4_e2m1fn_x4
 MAX = mybir.AluOpType.max
 MIN = mybir.AluOpType.min
+ADD = mybir.AluOpType.add
+SUB = mybir.AluOpType.subtract
 GELU = mybir.ActivationFunctionType.Gelu_apprx_tanh
 
 P = 128
@@ -22,7 +24,7 @@ PACK = 4
 PASSES = K // (P * PACK)
 ROWS = 16
 GROUP = 128
-PIECES = ((512, 512), (384, 384, 256))
+PIECES = (384, 384, 256)
 HALF = V // 2
 
 
@@ -48,12 +50,12 @@ def tile_picked_median_gelu_p_kernel(
         w_raw = keep.tile([P, PASSES, PACK, M], F32, name="w_raw")
         nc.sync.dma_start(word_table[0][:].bitcast(I32), x_words[0].bitcast(I32))
         nc.sync.dma_start(w_raw[:], w1.rearrange("(z p j) m -> p z j m", z=PASSES, j=PACK))
-        nc.sync.dma_start(word_table[1][:].bitcast(I32), x_words[1].bitcast(I32))
         pos_sb = []
         for d, pos in enumerate((pos1, pos2, pos3)):
             pos_tile = keep.tile([P, V // 16], U16, name=f"pos_sb{d}")
             nc.sync.dma_start(pos_tile[:], pos)
             pos_sb.append(pos_tile)
+        nc.sync.dma_start(word_table[1][:].bitcast(I32), x_words[1].bitcast(I32))
 
         x_plane = [keep.tile([P, S], U8, name=f"x_plane{z}", align_bytes=64) for z in range(PASSES)]
         for z in range(PASSES):
@@ -79,11 +81,8 @@ def tile_picked_median_gelu_p_kernel(
         banks = [psum.tile([M, GROUP], F32, name=f"bank{g}") for g in range(S // GROUP)]
         y = keep.tile([P, S], F32, name="y")
 
-        codes0 = []
-        first = 0
-        for width in PIECES[0]:
-            codes0.append((first, width, gather_words(0, first, width, f"codes0_{first}")))
-            first = first + width
+        spans = [(sum(PIECES[:i]), PIECES[i]) for i in range(len(PIECES))]
+        codes0 = [gather_words(0, first, width, f"codes0_{first}") for first, width in spans[:-1]]
 
         w_bf = keep.tile([P, PASSES, M, PACK], BF16, name="w_bf", tag="w_bf", align_bytes=64)
         nc.scalar.copy(w_bf[:], w_raw[:].rearrange("p z j m -> p z m j"))
@@ -108,31 +107,30 @@ def tile_picked_median_gelu_p_kernel(
                 if z == PASSES - 1:
                     nc.scalar.activation(y[:, g * GROUP : (g + 1) * GROUP], banks[g][:], GELU)
 
-        for first, width, codes in codes0:
+        codes0.append(gather_words(0, spans[-1][0], spans[-1][1], "w_bf"))
+        for (first, width), codes in zip(spans, codes0):
             multiply(0, first, width, codes)
-        first = 0
-        for width in PIECES[1]:
-            tag = "w_bf" if first == 0 else f"codes1_{first}"
-            multiply(1, first, width, gather_words(1, first, width, tag))
-            first = first + width
+        for first, width in spans:
+            multiply(1, first, width, gather_words(1, first, width, f"codes1_{first}"))
 
-        nb = []
-        for d in range(3):
-            fetched = keep.tile([P, V], F32, name=f"fetched{d}")
-            nc.vector.tensor_copy(fetched[:], y[:].indirect(pos_sb[d][:]))
-            nb.append(fetched)
-        hi = [keep.tile([P, HALF], F32, name=f"hi{h}") for h in range(2)]
-        lo = [keep.tile([P, HALF], F32, name=f"lo{h}") for h in range(2)]
-        cut = [keep.tile([P, HALF], F32, name=f"cut{h}") for h in range(2)]
-        med = [keep.tile([P, HALF], F32, name=f"med{h}") for h in range(2)]
-        cols = [slice(h * HALF, (h + 1) * HALF) for h in range(2)]
-        nc.vector.tensor_tensor(hi[0][:], nb[0][:, cols[0]], nb[1][:, cols[0]], MAX)
-        nc.vector.tensor_tensor(lo[0][:], nb[0][:, cols[0]], nb[1][:, cols[0]], MIN)
-        nc.vector.tensor_tensor(cut[0][:], hi[0][:], nb[2][:, cols[0]], MIN)
-        nc.vector.tensor_tensor(hi[1][:], nb[0][:, cols[1]], nb[1][:, cols[1]], MAX)
-        nc.vector.tensor_tensor(med[0][:], lo[0][:], cut[0][:], MAX)
-        nc.sync.dma_start(out[:, cols[0]], med[0][:])
-        nc.vector.tensor_tensor(cut[1][:], hi[1][:], nb[2][:, cols[1]], MIN)
-        nc.vector.tensor_tensor(lo[1][:], nb[0][:, cols[1]], nb[1][:, cols[1]], MIN)
-        nc.vector.tensor_tensor(med[1][:], lo[1][:], cut[1][:], MAX)
-        nc.sync.dma_start(out[:, cols[1]], med[1][:])
+        halves = range(2)
+        cols = [slice(h * HALF, (h + 1) * HALF) for h in halves]
+        entries = [slice(h * HALF // 16, (h + 1) * HALF // 16) for h in halves]
+
+        def pair(name):
+            return [keep.tile([P, HALF], F32, name=f"{name}{h}") for h in halves]
+
+        base, d1, d2, cut, shift, med = [pair(n) for n in ("base", "d1_", "d2_", "cut", "shift", "med")]
+        for h in halves:
+            nc.vector.tensor_copy(base[h][:], y[:].indirect(pos_sb[0][:, entries[h]]))
+        for h in halves:
+            nc.vector.tensor_tensor(d1[h][:], y[:].indirect(pos_sb[1][:, entries[h]]), base[h][:], SUB)
+        for h in halves:
+            nc.vector.tensor_tensor(d2[h][:], y[:].indirect(pos_sb[2][:, entries[h]]), base[h][:], SUB)
+        for h in halves:
+            nc.vector.scalar_tensor_tensor(cut[h][:], d1[h][:], 0.0, d2[h][:], MAX, MIN)
+        for h in halves:
+            nc.vector.scalar_tensor_tensor(shift[h][:], d1[h][:], 0.0, cut[h][:], MIN, MAX)
+        for h in halves:
+            nc.vector.tensor_tensor(med[h][:], shift[h][:], base[h][:], ADD)
+            nc.sync.dma_start(out[:, cols[h]], med[h][:])

@@ -47,7 +47,7 @@ def tile_picked_median_gelu_p_kernel(
         nc.vector.memset(scale_table[64:128, :].bitcast(I32), 0)
 
         word_table = [keep.tile([P, T], U16, name=f"word_table{z}", align_bytes=64) for z in range(PASSES)]
-        w_raw = keep.tile([P, PASSES, PACK, M], F32, name="w_raw")
+        w_raw = keep.tile([P, PASSES, PACK, M], F32, name="w_raw", tag="w_raw", align_bytes=64)
         nc.sync.dma_start(word_table[0][:].bitcast(I32), x_words[0].bitcast(I32))
         nc.sync.dma_start(w_raw[:], w1.rearrange("(z p j) m -> p z j m", z=PASSES, j=PACK))
         pos_sb = []
@@ -71,20 +71,21 @@ def tile_picked_median_gelu_p_kernel(
                     picked_scales[row : row + 4, :].bitcast(I32),
                 )
 
-        def gather_words(z, first, width, tag):
-            codes = keep.tile([P, width], U16, name=f"x_codes{z}_{first}", tag=tag, align_bytes=64)
+        def gather_words(z, first, width, codes):
             nc.vector.tensor_copy(
-                codes[:], word_table[z][:].indirect(offs_sb[:, first // 16 : (first + width) // 16])
+                codes, word_table[z][:].indirect(offs_sb[:, first // 16 : (first + width) // 16])
             )
-            return codes
 
         banks = [psum.tile([M, GROUP], F32, name=f"bank{g}") for g in range(S // GROUP)]
         y = keep.tile([P, S], F32, name="y")
 
         spans = [(sum(PIECES[:i]), PIECES[i]) for i in range(len(PIECES))]
-        codes0 = [gather_words(0, first, width, f"codes0_{first}") for first, width in spans[:-1]]
+        early = spans[-1][0]
+        early_codes = keep.tile([P, early], U16, name="early_codes", align_bytes=64)
+        for first, width in spans[:-1]:
+            gather_words(0, first, width, early_codes[:, first : first + width])
 
-        w_bf = keep.tile([P, PASSES, M, PACK], BF16, name="w_bf", tag="w_bf", align_bytes=64)
+        w_bf = keep.tile([P, PASSES, M, PACK], BF16, name="w_bf", align_bytes=64)
         nc.scalar.copy(w_bf[:], w_raw[:].rearrange("p z j m -> p z m j"))
         w_codes = keep.tile([P, PASSES * M], U32, name="w_codes", align_bytes=64)
         w_plane = keep.tile([P, PASSES * M], U8, name="w_plane", align_bytes=64)
@@ -107,11 +108,13 @@ def tile_picked_median_gelu_p_kernel(
                 if z == PASSES - 1:
                     nc.scalar.activation(y[:, g * GROUP : (g + 1) * GROUP], banks[g][:], GELU)
 
-        codes0.append(gather_words(0, spans[-1][0], spans[-1][1], "w_bf"))
-        for (first, width), codes in zip(spans, codes0):
-            multiply(0, first, width, codes)
-        for first, width in spans:
-            multiply(1, first, width, gather_words(1, first, width, f"codes1_{first}"))
+        late_codes = keep.tile([P, PASSES * S - early], U16, name="late_codes", tag="w_raw", align_bytes=64)
+        for first, width in spans[:-1]:
+            multiply(0, first, width, early_codes[:, first : first + width])
+        for z, first, width in [(0,) + spans[-1]] + [(1,) + span for span in spans]:
+            at = z * S + first - early
+            gather_words(z, first, width, late_codes[:, at : at + width])
+            multiply(z, first, width, late_codes[:, at : at + width])
 
         halves = range(2)
         cols = [slice(h * HALF, (h + 1) * HALF) for h in halves]

@@ -22,7 +22,10 @@ GELU = mybir.ActivationFunctionType.Gelu_apprx_tanh
 P = 128
 PACK = 4
 PASSES = K // (P * PACK)
-ROWS = 16
+BLOCKS = 16
+QUADRANT = 32
+QUADRANT_ROWS = BLOCKS * QUADRANT // P
+STRIPE = 16
 GROUP = 128
 PIECES = (384, 384, 256)
 HALF = V // 2
@@ -36,23 +39,28 @@ def tile_picked_median_gelu_p_kernel(
         keep = ctx.enter_context(tc.tile_pool(name="keep", bufs=1))
         psum = ctx.enter_context(tc.psum_pool(name="psum", bufs=1))
 
+        scale_rows = PASSES * BLOCKS
         scale_table = keep.tile([P, T], U8, name="scale_table", align_bytes=64)
         nc.sync.dma_start(
-            scale_table[0 : PASSES * ROWS, :].bitcast(I32),
+            scale_table[0:scale_rows, :].bitcast(I32),
             x_scales.rearrange("z q c -> (z q) c").bitcast(I32),
         )
-        offs_sb = keep.tile([P, S // 16], U16, name="offs_sb")
+        offs_sb = keep.tile([P, S // STRIPE], U16, name="offs_sb")
         nc.sync.dma_start(offs_sb[:], offs)
-        nc.vector.memset(scale_table[32:64, :].bitcast(I32), 0)
-        nc.vector.memset(scale_table[64:128, :].bitcast(I32), 0)
+        nc.vector.memset(scale_table[scale_rows : P // 2, :].bitcast(I32), 0)
+        nc.vector.memset(scale_table[P // 2 : P, :].bitcast(I32), 0)
 
         word_table = [keep.tile([P, T], U16, name=f"word_table{z}", align_bytes=64) for z in range(PASSES)]
-        w_raw = keep.tile([P, PASSES, PACK, M], F32, name="w_raw", tag="w_raw", align_bytes=64)
+        w_raw = [keep.tile([P, PACK, M], F32, name=f"w_raw{z}", tag=f"w_raw{z}", align_bytes=64) for z in range(PASSES)]
+        warm = keep.tile([P, 2], F32, name="warm")
+        nc.vector.memset(warm[:, 0:1], 0.0)
+        nc.scalar.activation(warm[:, 1:2], warm[:, 0:1], GELU)
         nc.sync.dma_start(word_table[0][:].bitcast(I32), x_words[0].bitcast(I32))
-        nc.sync.dma_start(w_raw[:], w1.rearrange("(z p j) m -> p z j m", z=PASSES, j=PACK))
+        for z in range(PASSES):
+            nc.sync.dma_start(w_raw[z][:], w1.rearrange("(z p j) m -> z p j m", z=PASSES, j=PACK)[z])
         pos_sb = []
         for d, pos in enumerate((pos1, pos2, pos3)):
-            pos_tile = keep.tile([P, V // 16], U16, name=f"pos_sb{d}")
+            pos_tile = keep.tile([P, V // STRIPE], U16, name=f"pos_sb{d}")
             nc.sync.dma_start(pos_tile[:], pos)
             pos_sb.append(pos_tile)
         nc.sync.dma_start(word_table[1][:].bitcast(I32), x_words[1].bitcast(I32))
@@ -64,16 +72,16 @@ def tile_picked_median_gelu_p_kernel(
         picked_scales = keep.tile([P, S], U8, name="picked_scales", align_bytes=64)
         nc.vector.tensor_copy(picked_scales[:], scale_table[:].indirect(offs_sb[:]))
         for z in range(PASSES):
-            for q in range(4):
-                row = ROWS * z + 4 * q
+            for q in range(P // QUADRANT):
+                row = BLOCKS * z + QUADRANT_ROWS * q
                 nc.sync.dma_start(
-                    x_plane[z][32 * q : 32 * q + 4, :].bitcast(I32),
-                    picked_scales[row : row + 4, :].bitcast(I32),
+                    x_plane[z][QUADRANT * q : QUADRANT * q + QUADRANT_ROWS, :].bitcast(I32),
+                    picked_scales[row : row + QUADRANT_ROWS, :].bitcast(I32),
                 )
 
         def gather_words(z, first, width, codes):
             nc.vector.tensor_copy(
-                codes, word_table[z][:].indirect(offs_sb[:, first // 16 : (first + width) // 16])
+                codes, word_table[z][:].indirect(offs_sb[:, first // STRIPE : (first + width) // STRIPE])
             )
 
         banks = [psum.tile([M, GROUP], F32, name=f"bank{g}") for g in range(S // GROUP)]
@@ -86,7 +94,10 @@ def tile_picked_median_gelu_p_kernel(
             gather_words(0, first, width, early_codes[:, first : first + width])
 
         w_bf = keep.tile([P, PASSES, M, PACK], BF16, name="w_bf", align_bytes=64)
-        nc.scalar.copy(w_bf[:], w_raw[:].rearrange("p z j m -> p z m j"))
+        for z in range(PASSES):
+            nc.scalar.copy(
+                w_bf[:, z].rearrange("p (c i) j -> p c j i", i=4), w_raw[z][:].rearrange("p j (c i) -> p c j i", i=4)
+            )
         w_codes = keep.tile([P, PASSES * M], U32, name="w_codes", align_bytes=64)
         w_plane = keep.tile([P, PASSES * M], U8, name="w_plane", align_bytes=64)
         nc.vector.quantize_mx(
@@ -108,7 +119,7 @@ def tile_picked_median_gelu_p_kernel(
                 if z == PASSES - 1:
                     nc.scalar.activation(y[:, g * GROUP : (g + 1) * GROUP], banks[g][:], GELU)
 
-        late_codes = keep.tile([P, PASSES * S - early], U16, name="late_codes", tag="w_raw", align_bytes=64)
+        late_codes = keep.tile([P, PASSES * S - early], U16, name="late_codes", tag="w_raw1", align_bytes=64)
         for first, width in spans[:-1]:
             multiply(0, first, width, early_codes[:, first : first + width])
         for z, first, width in [(0,) + spans[-1]] + [(1,) + span for span in spans]:
@@ -116,9 +127,9 @@ def tile_picked_median_gelu_p_kernel(
             gather_words(z, first, width, late_codes[:, at : at + width])
             multiply(z, first, width, late_codes[:, at : at + width])
 
-        halves = range(2)
+        halves = range(V // HALF)
         cols = [slice(h * HALF, (h + 1) * HALF) for h in halves]
-        entries = [slice(h * HALF // 16, (h + 1) * HALF // 16) for h in halves]
+        entries = [slice(h * HALF // STRIPE, (h + 1) * HALF // STRIPE) for h in halves]
 
         def pair(name):
             return [keep.tile([P, HALF], F32, name=f"{name}{h}") for h in halves]
@@ -134,6 +145,8 @@ def tile_picked_median_gelu_p_kernel(
             nc.vector.scalar_tensor_tensor(cut[h][:], d1[h][:], 0.0, d2[h][:], MAX, MIN)
         for h in halves:
             nc.vector.scalar_tensor_tensor(shift[h][:], d1[h][:], 0.0, cut[h][:], MIN, MAX)
-        for h in halves:
-            nc.vector.tensor_tensor(med[h][:], shift[h][:], base[h][:], ADD)
-            nc.sync.dma_start(out[:, cols[h]], med[h][:])
+        nc.vector.tensor_tensor(med[0][:], shift[0][:], base[0][:], ADD)
+        nc.sync.dma_start(out[:, cols[0]], med[0][:])
+        for a, b in ((0, 128), (128, 256)):
+            nc.vector.tensor_tensor(med[1][:, a:b], shift[1][:, a:b], base[1][:, a:b], ADD)
+            nc.sync.dma_start(out[:, HALF + a : HALF + b], med[1][:, a:b])

@@ -42,13 +42,12 @@ def tile_picked_median_gelu_p_kernel(
         scale_rows = PASSES * BLOCKS
         scale_table = keep.tile([P, T], U8, name="scale_table", align_bytes=64)
         nc.sync.dma_start(
-            scale_table[0:scale_rows, :].bitcast(I32),
+            scale_table[P - scale_rows : P, :].bitcast(I32),
             x_scales.rearrange("z q c -> (z q) c").bitcast(I32),
         )
         offs_sb = keep.tile([P, S // STRIPE], U16, name="offs_sb")
         nc.sync.dma_start(offs_sb[:], offs)
-        nc.vector.memset(scale_table[scale_rows : P // 2, :].bitcast(I32), 0)
-        nc.vector.memset(scale_table[P // 2 : P, :].bitcast(I32), 0)
+        nc.vector.memset(scale_table[0 : P - scale_rows, :].bitcast(I32), 0)
 
         word_table = [keep.tile([P, T], U16, name=f"word_table{z}", align_bytes=64) for z in range(PASSES)]
         w_raw = [keep.tile([P, PACK, M], F32, name=f"w_raw{z}", tag=f"w_raw{z}", align_bytes=64) for z in range(PASSES)]
@@ -65,15 +64,15 @@ def tile_picked_median_gelu_p_kernel(
             pos_sb.append(pos_tile)
         nc.sync.dma_start(word_table[1][:].bitcast(I32), x_words[1].bitcast(I32))
 
-        x_plane = [keep.tile([P, S], U8, name=f"x_plane{z}", align_bytes=64) for z in range(PASSES)]
-        for z in range(PASSES):
-            nc.vector.memset(x_plane[z][:].bitcast(I32), 0)
+        x_planes = keep.tile([P, PASSES * S], U8, name="x_planes", align_bytes=64)
+        nc.vector.memset(x_planes[:].bitcast(I32), 0)
+        x_plane = [x_planes[:, z * S : (z + 1) * S] for z in range(PASSES)]
 
         picked_scales = keep.tile([P, S], U8, name="picked_scales", align_bytes=64)
         nc.vector.tensor_copy(picked_scales[:], scale_table[:].indirect(offs_sb[:]))
         for z in range(PASSES):
             for q in range(P // QUADRANT):
-                row = BLOCKS * z + QUADRANT_ROWS * q
+                row = P - scale_rows + BLOCKS * z + QUADRANT_ROWS * q
                 nc.sync.dma_start(
                     x_plane[z][QUADRANT * q : QUADRANT * q + QUADRANT_ROWS, :].bitcast(I32),
                     picked_scales[row : row + QUADRANT_ROWS, :].bitcast(I32),

@@ -54,14 +54,14 @@ def tile_picked_median_gelu_p_kernel(
         warm = keep.tile([P, 2], F32, name="warm")
         nc.vector.memset(warm[:, 0:1], 0.0)
         nc.scalar.activation(warm[:, 1:2], warm[:, 0:1], GELU)
-        nc.sync.dma_start(word_table[0][:].bitcast(I32), x_words[0].bitcast(I32))
-        for z in range(PASSES):
-            nc.sync.dma_start(w_raw[z][:], w1.rearrange("(z p j) m -> z p j m", z=PASSES, j=PACK)[z])
         pos_sb = []
         for d, pos in enumerate((pos1, pos2, pos3)):
             pos_tile = keep.tile([P, V // STRIPE], U16, name=f"pos_sb{d}")
             nc.sync.dma_start(pos_tile[:], pos)
             pos_sb.append(pos_tile)
+        nc.sync.dma_start(word_table[0][:].bitcast(I32), x_words[0].bitcast(I32))
+        for z in range(PASSES):
+            nc.sync.dma_start(w_raw[z][:], w1.rearrange("(z p j) m -> z p j m", z=PASSES, j=PACK)[z])
         nc.sync.dma_start(word_table[1][:].bitcast(I32), x_words[1].bitcast(I32))
 
         x_planes = keep.tile([P, PASSES * S], U8, name="x_planes", align_bytes=64)
@@ -133,13 +133,16 @@ def tile_picked_median_gelu_p_kernel(
         def pair(name):
             return [keep.tile([P, HALF], F32, name=f"{name}{h}") for h in halves]
 
-        base, d1, d2, cut, shift, med = [pair(n) for n in ("base", "d1_", "d2_", "cut", "shift", "med")]
+        d1, cut, shift, med = [pair(n) for n in ("d1_", "cut", "shift", "med")]
+        base_all = keep.tile([P, V], F32, name="base_all")
+        d2_all = keep.tile([P, V], F32, name="d2_all")
+        base = [base_all[:, c] for c in cols]
+        d2 = [d2_all[:, c] for c in cols]
         for h in halves:
             nc.vector.tensor_copy(base[h][:], y[:].indirect(pos_sb[0][:, entries[h]]))
-        for h in halves:
-            nc.vector.tensor_tensor(d1[h][:], y[:].indirect(pos_sb[1][:, entries[h]]), base[h][:], SUB)
-        for h in halves:
-            nc.vector.tensor_tensor(d2[h][:], y[:].indirect(pos_sb[2][:, entries[h]]), base[h][:], SUB)
+        nc.vector.tensor_tensor(d1[0][:], y[:].indirect(pos_sb[1][:, entries[0]]), base[0][:], SUB)
+        nc.vector.tensor_tensor(d2_all[:], y[:].indirect(pos_sb[2][:]), base_all[:], SUB)
+        nc.vector.tensor_tensor(d1[1][:], y[:].indirect(pos_sb[1][:, entries[1]]), base[1][:], SUB)
         for h in halves:
             nc.vector.scalar_tensor_tensor(cut[h][:], d1[h][:], 0.0, d2[h][:], MAX, MIN)
         for h in halves:

@@ -28,7 +28,7 @@ QUADRANT_ROWS = BLOCKS * QUADRANT // P
 STRIPE = 16
 GROUP = 128
 PIECES = (384, 384, 256)
-HALF = V // 2
+PARTS = (192, 192, 128)
 
 
 def tile_picked_median_gelu_p_kernel(
@@ -126,29 +126,25 @@ def tile_picked_median_gelu_p_kernel(
             gather_words(z, first, width, late_codes[:, at : at + width])
             multiply(z, first, width, late_codes[:, at : at + width])
 
-        halves = range(V // HALF)
-        cols = [slice(h * HALF, (h + 1) * HALF) for h in halves]
-        entries = [slice(h * HALF // STRIPE, (h + 1) * HALF // STRIPE) for h in halves]
+        def whole(name):
+            return keep.tile([P, V], F32, name=name)
 
-        def pair(name):
-            return [keep.tile([P, HALF], F32, name=f"{name}{h}") for h in halves]
+        def entries(d, a, b):
+            return y[:].indirect(pos_sb[d][:, a // STRIPE : b // STRIPE])
 
-        d1, cut, shift, med = [pair(n) for n in ("d1_", "cut", "shift", "med")]
-        base_all = keep.tile([P, V], F32, name="base_all")
-        d2_all = keep.tile([P, V], F32, name="d2_all")
-        base = [base_all[:, c] for c in cols]
-        d2 = [d2_all[:, c] for c in cols]
-        for h in halves:
-            nc.vector.tensor_copy(base[h][:], y[:].indirect(pos_sb[0][:, entries[h]]))
-        nc.vector.tensor_tensor(d1[0][:], y[:].indirect(pos_sb[1][:, entries[0]]), base[0][:], SUB)
-        nc.vector.tensor_tensor(d2_all[:], y[:].indirect(pos_sb[2][:]), base_all[:], SUB)
-        nc.vector.tensor_tensor(d1[1][:], y[:].indirect(pos_sb[1][:, entries[1]]), base[1][:], SUB)
-        for h in halves:
-            nc.vector.scalar_tensor_tensor(cut[h][:], d1[h][:], 0.0, d2[h][:], MAX, MIN)
-        for h in halves:
-            nc.vector.scalar_tensor_tensor(shift[h][:], d1[h][:], 0.0, cut[h][:], MIN, MAX)
-        nc.vector.tensor_tensor(med[0][:], shift[0][:], base[0][:], ADD)
-        nc.sync.dma_start(out[:, cols[0]], med[0][:])
-        for a, b in ((0, 128), (128, 256)):
-            nc.vector.tensor_tensor(med[1][:, a:b], shift[1][:, a:b], base[1][:, a:b], ADD)
-            nc.sync.dma_start(out[:, HALF + a : HALF + b], med[1][:, a:b])
+        base, d1, d2, cut, shift = [whole(n) for n in ("base", "d1", "d2", "cut", "shift")]
+        parts = [(sum(PARTS[:i]), sum(PARTS[: i + 1])) for i in range(len(PARTS))]
+        last = parts[-1][0]
+        nc.vector.tensor_copy(base[:, :last], entries(0, 0, last))
+        nc.vector.tensor_copy(base[:, last:], entries(0, last, V))
+        nc.vector.tensor_tensor(d1[:, :last], entries(1, 0, last), base[:, :last], SUB)
+        nc.vector.tensor_tensor(d2[:], entries(2, 0, V), base[:], SUB)
+        nc.vector.tensor_tensor(d1[:, last:], entries(1, last, V), base[:, last:], SUB)
+        for a, b in parts:
+            nc.vector.scalar_tensor_tensor(cut[:, a:b], d1[:, a:b], 0.0, d2[:, a:b], MAX, MIN)
+        for a, b in parts:
+            nc.vector.scalar_tensor_tensor(shift[:, a:b], d1[:, a:b], 0.0, cut[:, a:b], MIN, MAX)
+        for i, (a, b) in enumerate(parts):
+            med = keep.tile([P, b - a], F32, name=f"med{i}")
+            nc.vector.tensor_tensor(med[:], shift[:, a:b], base[:, a:b], ADD)
+            nc.sync.dma_start(out[:, a:b], med[:])

@@ -1,6 +1,7 @@
 from contextlib import ExitStack
 
 import concourse.mybir as mybir
+from concourse.masks import make_identity
 
 K, T, S, V, M = 1024, 2048, 1024, 512, 128
 FLOPS = 2 * K * M * S
@@ -17,6 +18,9 @@ MAX = mybir.AluOpType.max
 MIN = mybir.AluOpType.min
 ADD = mybir.AluOpType.add
 SUB = mybir.AluOpType.subtract
+RELU = mybir.ActivationFunctionType.Relu
+COPY = mybir.ActivationFunctionType.Copy
+MULT = mybir.AluOpType.mult
 GELU = mybir.ActivationFunctionType.Gelu_apprx_tanh
 
 P = 128
@@ -28,7 +32,7 @@ QUADRANT_ROWS = BLOCKS * QUADRANT // P
 STRIPE = 16
 GROUP = 128
 PIECES = (384, 384, 256)
-PARTS = (192, 192, 128)
+BOUND_BLOCKS = 3
 
 
 def tile_picked_median_gelu_p_kernel(
@@ -64,6 +68,9 @@ def tile_picked_median_gelu_p_kernel(
             nc.sync.dma_start(w_raw[z][:], w1.rearrange("(z p j) m -> z p j m", z=PASSES, j=PACK)[z])
         nc.sync.dma_start(word_table[1][:].bitcast(I32), x_words[1].bitcast(I32))
 
+        ident = keep.tile([P, P], F32, name="ident")
+        make_identity(nc, ident[:])
+
         x_planes = keep.tile([P, PASSES * S], U8, name="x_planes", align_bytes=64)
         nc.vector.memset(x_planes[:].bitcast(I32), 0)
         x_plane = [x_planes[:, z * S : (z + 1) * S] for z in range(PASSES)]
@@ -83,7 +90,7 @@ def tile_picked_median_gelu_p_kernel(
                 codes, word_table[z][:].indirect(offs_sb[:, first // STRIPE : (first + width) // STRIPE])
             )
 
-        banks = [psum.tile([M, GROUP], F32, name=f"bank{g}") for g in range(S // GROUP)]
+        banks = [psum.tile([M, GROUP], F32, name=f"bank{g}", tag=f"bank{g}") for g in range(S // GROUP)]
         y = keep.tile([P, S], F32, name="y")
 
         spans = [(sum(PIECES[:i]), PIECES[i]) for i in range(len(PIECES))]
@@ -126,25 +133,76 @@ def tile_picked_median_gelu_p_kernel(
             gather_words(z, first, width, late_codes[:, at : at + width])
             multiply(z, first, width, late_codes[:, at : at + width])
 
-        def whole(name):
-            return keep.tile([P, V], F32, name=name)
-
         def entries(d, a, b):
             return y[:].indirect(pos_sb[d][:, a // STRIPE : b // STRIPE])
 
-        base, d1, d2, cut, shift = [whole(n) for n in ("base", "d1", "d2", "cut", "shift")]
-        parts = [(sum(PARTS[:i]), sum(PARTS[: i + 1])) for i in range(len(PARTS))]
-        last = parts[-1][0]
-        nc.vector.tensor_copy(base[:, :last], entries(0, 0, last))
-        nc.vector.tensor_copy(base[:, last:], entries(0, last, V))
-        nc.vector.tensor_tensor(d1[:, :last], entries(1, 0, last), base[:, :last], SUB)
-        nc.vector.tensor_tensor(d2[:], entries(2, 0, V), base[:], SUB)
-        nc.vector.tensor_tensor(d1[:, last:], entries(1, last, V), base[:, last:], SUB)
-        for a, b in parts:
-            nc.vector.scalar_tensor_tensor(cut[:, a:b], d1[:, a:b], 0.0, d2[:, a:b], MAX, MIN)
-        for a, b in parts:
-            nc.vector.scalar_tensor_tensor(shift[:, a:b], d1[:, a:b], 0.0, cut[:, a:b], MIN, MAX)
-        for i, (a, b) in enumerate(parts):
-            med = keep.tile([P, b - a], F32, name=f"med{i}")
-            nc.vector.tensor_tensor(med[:], shift[:, a:b], base[:, a:b], ADD)
+        def turn(bank, block, start, stop):
+            nc.tensor.matmul(bank, lhsT=block, rhs=ident[:], is_transpose=True, start=start, stop=stop)
+
+        first = BOUND_BLOCKS * P
+        rest = V - first
+        half = first // 2
+        last_block = BOUND_BLOCKS - 1
+        blocks = [slice(j * P, (j + 1) * P) for j in range(BOUND_BLOCKS)]
+        a_spans = [(0, last_block), (last_block, BOUND_BLOCKS)]
+        a_first = [keep.tile([P, (e - b) * P], F32, name=f"a_first{i}", tag=f"a_first{i}") for i, (b, e) in enumerate(a_spans)]
+        a_rest = keep.tile([P, rest], F32, name="a_rest")
+        d1_first = [keep.tile([P, (e - b) * P], F32, name=f"d1_first{i}", tag=f"d1_first{i}") for i, (b, e) in enumerate(a_spans)]
+        d1_rest = keep.tile([P, rest], F32, name="d1_rest")
+        d2_rest = keep.tile([P, rest], F32, name="d2_rest")
+        for i, (b, e) in enumerate(a_spans):
+            nc.vector.tensor_copy(a_first[i][:], entries(0, b * P, e * P))
+        nc.vector.tensor_copy(a_rest[:], entries(0, first, V))
+        for i, (b, e) in enumerate(a_spans):
+            nc.vector.tensor_tensor(d1_first[i][:], entries(1, b * P, e * P), a_first[i][:], SUB)
+        nc.vector.tensor_tensor(d1_rest[:], entries(1, first, V), a_rest[:], SUB)
+        nc.vector.tensor_tensor(d2_rest[:], entries(2, first, V), a_rest[:], SUB)
+
+        a_bank = [psum.tile([P, (e - b) * P], F32, name=f"a_bank{i}", tag=f"bank{i}") for i, (b, e) in enumerate(a_spans)]
+        d_bank = [psum.tile([P, P], F32, name=f"d_bank{j}", tag=f"bank{2 + j}") for j in range(BOUND_BLOCKS)]
+        high = psum.tile([P, first], F32, name="high", tag="bank6")
+        low = psum.tile([P, first], F32, name="low", tag="bank7")
+        a_t = keep.tile([P, first], F32, name="a_t")
+        minus_a_t = keep.tile([P, first], F32, name="minus_a_t")
+        up_t = keep.tile([P, first], F32, name="up_t", tag="up_t")
+        down_t = keep.tile([P, first], F32, name="down_t", tag="down_t")
+        for i, (b, e) in enumerate(a_spans):
+            for j in range(b, e):
+                turn(a_bank[i][:, blocks[j - b]], a_first[i][:, blocks[j - b]], True, True)
+            nc.scalar.copy(a_t[:, b * P : e * P], a_bank[i][:])
+        for i, (b, e) in enumerate(a_spans):
+            nc.scalar.activation(minus_a_t[:, b * P : e * P], a_bank[i][:], COPY, scale=-1.0)
+        for j, s in enumerate(blocks):
+            turn(high[:, s], a_t[:, s], j == 0, False)
+        for i, (b, e) in enumerate(a_spans):
+            for j in range(b, e):
+                turn(d_bank[j][:], d1_first[i][:, blocks[j - b]], True, True)
+        for j, s in enumerate(blocks):
+            nc.scalar.activation(up_t[:, s], d_bank[j][:], RELU)
+        for j, s in enumerate(blocks):
+            turn(high[:, s], up_t[:, s], False, j == last_block)
+        for j, s in enumerate(blocks):
+            turn(low[:, s], minus_a_t[:, s], j == 0, False)
+        for j, s in enumerate(blocks):
+            nc.scalar.activation(down_t[:, s], d_bank[j][:], RELU, scale=-1.0)
+        for j, s in enumerate(blocks):
+            turn(low[:, s], down_t[:, s], False, j == last_block)
+
+        halves = [(0, half), (half, first)]
+        c_first = [keep.tile([P, half], F32, name=f"c_first{i}", tag=tag) for i, tag in enumerate(("a_first0", "d1_first0"))]
+        cut = keep.tile([P, rest], F32, name="cut")
+        shift = keep.tile([P, rest], F32, name="shift")
+        capped = keep.tile([P, first], F32, name="capped")
+        nc.vector.tensor_copy(c_first[0][:], entries(2, 0, half))
+        nc.vector.scalar_tensor_tensor(cut[:], d1_rest[:], 0.0, d2_rest[:], MAX, MIN)
+        nc.vector.tensor_copy(c_first[1][:], entries(2, half, first))
+        nc.vector.scalar_tensor_tensor(shift[:], d1_rest[:], 0.0, cut[:], MIN, MAX)
+        for i, (a, b) in enumerate(halves):
+            nc.vector.tensor_tensor(capped[:, a:b], high[:, a:b], c_first[i][:], MIN)
+        med_rest = keep.tile([P, rest], F32, name="med_rest", tag="up_t")
+        nc.vector.tensor_tensor(med_rest[:], shift[:], a_rest[:], ADD)
+        nc.sync.dma_start(out[:, first:], med_rest[:])
+        for i, (a, b) in enumerate(halves):
+            med = keep.tile([P, half], F32, name=f"med{i}")
+            nc.vector.scalar_tensor_tensor(med[:], low[:, a:b], -1.0, capped[:, a:b], MULT, MAX)
             nc.sync.dma_start(out[:, a:b], med[:])

@@ -141,27 +141,27 @@ def tile_picked_median_gelu_p_kernel(
 
         first = BOUND_BLOCKS * P
         rest = V - first
-        half = first // 2
         last_block = BOUND_BLOCKS - 1
         blocks = [slice(j * P, (j + 1) * P) for j in range(BOUND_BLOCKS)]
         a_spans = [(0, last_block), (last_block, BOUND_BLOCKS)]
-        a_first = [keep.tile([P, (e - b) * P], F32, name=f"a_first{i}", tag=f"a_first{i}") for i, (b, e) in enumerate(a_spans)]
-        a_rest = keep.tile([P, rest], F32, name="a_rest")
-        d1_first = [keep.tile([P, (e - b) * P], F32, name=f"d1_first{i}", tag=f"d1_first{i}") for i, (b, e) in enumerate(a_spans)]
-        d1_rest = keep.tile([P, rest], F32, name="d1_rest")
-        d2_rest = keep.tile([P, rest], F32, name="d2_rest")
-        for i, (b, e) in enumerate(a_spans):
-            nc.vector.tensor_copy(a_first[i][:], entries(0, b * P, e * P))
-        nc.vector.tensor_copy(a_rest[:], entries(0, first, V))
-        for i, (b, e) in enumerate(a_spans):
-            nc.vector.tensor_tensor(d1_first[i][:], entries(1, b * P, e * P), a_first[i][:], SUB)
-        nc.vector.tensor_tensor(d1_rest[:], entries(1, first, V), a_rest[:], SUB)
-        nc.vector.tensor_tensor(d2_rest[:], entries(2, first, V), a_rest[:], SUB)
+        mid = V // 2
+        a_half = [keep.tile([P, mid], F32, name=f"a_half{i}", tag=f"a_first{i}") for i in range(2)]
+        a_first = [a_half[0][:], a_half[1][:, : first - mid]]
+        a_rest = a_half[1][:, first - mid :]
+        d1_half = [keep.tile([P, mid], F32, name=f"d1_half{i}", tag=f"d1_first{i}") for i in range(2)]
+        d1_first = [d1_half[0][:], d1_half[1][:, : first - mid]]
+        d1_rest = d1_half[1][:, first - mid :]
+        d2_rest = keep.tile([P, rest], F32, name="d2_rest", tag="d2_rest")
+        for i in range(2):
+            nc.vector.tensor_copy(a_half[i][:], entries(0, i * mid, (i + 1) * mid))
+        for i in range(2):
+            nc.vector.tensor_tensor(d1_half[i][:], entries(1, i * mid, (i + 1) * mid), a_half[i][:], SUB)
+        nc.vector.tensor_tensor(d2_rest[:], entries(2, first, V), a_rest, SUB)
 
         a_bank = [psum.tile([P, (e - b) * P], F32, name=f"a_bank{i}", tag=f"bank{i}") for i, (b, e) in enumerate(a_spans)]
         d_bank = [psum.tile([P, P], F32, name=f"d_bank{j}", tag=f"bank{2 + j}") for j in range(BOUND_BLOCKS)]
-        high = psum.tile([P, first], F32, name="high", tag="bank6")
-        low = psum.tile([P, first], F32, name="low", tag="bank7")
+        high = [psum.tile([P, P], F32, name=f"high{j}", tag=f"bank{5 + j}") for j in range(BOUND_BLOCKS)]
+        low = [psum.tile([P, P], F32, name=f"low{j}", tag=f"bank{j}") for j in range(BOUND_BLOCKS)]
         a_t = keep.tile([P, first], F32, name="a_t")
         minus_a_t = keep.tile([P, first], F32, name="minus_a_t")
         up_t = keep.tile([P, first], F32, name="up_t", tag="up_t")
@@ -173,36 +173,35 @@ def tile_picked_median_gelu_p_kernel(
         for i, (b, e) in enumerate(a_spans):
             nc.scalar.activation(minus_a_t[:, b * P : e * P], a_bank[i][:], COPY, scale=-1.0)
         for j, s in enumerate(blocks):
-            turn(high[:, s], a_t[:, s], j == 0, False)
+            turn(high[j][:], a_t[:, s], True, False)
         for i, (b, e) in enumerate(a_spans):
             for j in range(b, e):
                 turn(d_bank[j][:], d1_first[i][:, blocks[j - b]], True, True)
         for j, s in enumerate(blocks):
             nc.scalar.activation(up_t[:, s], d_bank[j][:], RELU)
         for j, s in enumerate(blocks):
-            turn(high[:, s], up_t[:, s], False, j == last_block)
-        for j, s in enumerate(blocks):
-            turn(low[:, s], minus_a_t[:, s], j == 0, False)
+            turn(high[j][:], up_t[:, s], False, True)
         for j, s in enumerate(blocks):
             nc.scalar.activation(down_t[:, s], d_bank[j][:], RELU, scale=-1.0)
         for j, s in enumerate(blocks):
-            turn(low[:, s], down_t[:, s], False, j == last_block)
+            turn(low[j][:], minus_a_t[:, s], True, False)
+            turn(low[j][:], down_t[:, s], False, True)
 
-        halves = [(0, half), (half, first)]
-        c_first = [keep.tile([P, half], F32, name=f"c_first{i}", tag=tag) for i, tag in enumerate(("a_first0", "d1_first0"))]
+        c_block = [keep.tile([P, P], F32, name=f"c_block{j}", tag=tag) for j, tag in enumerate(("a_first0", "d1_first0", "d2_rest"))]
         cut = keep.tile([P, rest], F32, name="cut")
         shift = keep.tile([P, rest], F32, name="shift")
         capped = keep.tile([P, first], F32, name="capped")
-        nc.vector.tensor_copy(c_first[0][:], entries(2, 0, half))
-        nc.vector.scalar_tensor_tensor(cut[:], d1_rest[:], 0.0, d2_rest[:], MAX, MIN)
-        nc.vector.tensor_copy(c_first[1][:], entries(2, half, first))
-        nc.vector.scalar_tensor_tensor(shift[:], d1_rest[:], 0.0, cut[:], MIN, MAX)
-        for i, (a, b) in enumerate(halves):
-            nc.vector.tensor_tensor(capped[:, a:b], high[:, a:b], c_first[i][:], MIN)
-        med_rest = keep.tile([P, rest], F32, name="med_rest", tag="up_t")
-        nc.vector.tensor_tensor(med_rest[:], shift[:], a_rest[:], ADD)
+        nc.vector.tensor_copy(c_block[0][:], entries(2, 0, P))
+        nc.vector.scalar_tensor_tensor(cut[:], d1_rest, 0.0, d2_rest[:], MAX, MIN)
+        nc.vector.tensor_copy(c_block[1][:], entries(2, P, 2 * P))
+        nc.vector.scalar_tensor_tensor(shift[:], d1_rest, 0.0, cut[:], MIN, MAX)
+        nc.vector.tensor_copy(c_block[2][:], entries(2, 2 * P, first))
+        for s, c, bound in zip(blocks, c_block, high):
+            nc.vector.tensor_tensor(capped[:, s], bound[:], c[:], MIN)
+        med_rest = keep.tile([P, rest], F32, name="med_rest")
+        nc.gpsimd.tensor_tensor(med_rest[:], shift[:], a_rest, ADD)
         nc.sync.dma_start(out[:, first:], med_rest[:])
-        for i, (a, b) in enumerate(halves):
-            med = keep.tile([P, half], F32, name=f"med{i}")
-            nc.vector.scalar_tensor_tensor(med[:], low[:, a:b], -1.0, capped[:, a:b], MULT, MAX)
-            nc.sync.dma_start(out[:, a:b], med[:])
+        for j, s in enumerate(blocks):
+            med = keep.tile([P, P], F32, name=f"med{j}")
+            nc.vector.scalar_tensor_tensor(med[:], low[j][:], -1.0, capped[:, s], MULT, MAX)
+            nc.sync.dma_start(out[:, s], med[:])

@@ -31,7 +31,7 @@ QUADRANT = 32
 QUADRANT_ROWS = BLOCKS * QUADRANT // P
 STRIPE = 16
 GROUP = 128
-PIECES = (384, 384, 256)
+PIECES = ((1024,), (384, 384, 256))
 BOUND_BLOCKS = 3
 
 
@@ -53,7 +53,8 @@ def tile_picked_median_gelu_p_kernel(
         nc.sync.dma_start(offs_sb[:], offs)
         nc.vector.memset(scale_table[0 : P - scale_rows, :].bitcast(I32), 0)
 
-        word_table = [keep.tile([P, T], U16, name=f"word_table{z}", align_bytes=64) for z in range(PASSES)]
+        word_table = [keep.tile([P, w], U16, name=f"word_table{z}", align_bytes=64) for z, w in enumerate((2 * T, T))]
+        nc.vector.memset(word_table[0][:, T:].bitcast(I32), 0)
         w_raw = [keep.tile([P, PACK, M], F32, name=f"w_raw{z}", tag=f"w_raw{z}", align_bytes=64) for z in range(PASSES)]
         warm = keep.tile([P, 2], F32, name="warm")
         nc.vector.memset(warm[:, 0:1], 0.0)
@@ -63,7 +64,7 @@ def tile_picked_median_gelu_p_kernel(
             pos_tile = keep.tile([P, V // STRIPE], U16, name=f"pos_sb{d}")
             nc.sync.dma_start(pos_tile[:], pos)
             pos_sb.append(pos_tile)
-        nc.sync.dma_start(word_table[0][:].bitcast(I32), x_words[0].bitcast(I32))
+        nc.sync.dma_start(word_table[0][:, :T].bitcast(I32), x_words[0].bitcast(I32))
         for z in range(PASSES):
             nc.sync.dma_start(w_raw[z][:], w1.rearrange("(z p j) m -> z p j m", z=PASSES, j=PACK)[z])
         nc.sync.dma_start(word_table[1][:].bitcast(I32), x_words[1].bitcast(I32))
@@ -93,10 +94,10 @@ def tile_picked_median_gelu_p_kernel(
         banks = [psum.tile([M, GROUP], F32, name=f"bank{g}", tag=f"bank{g}") for g in range(S // GROUP)]
         y = keep.tile([P, S], F32, name="y")
 
-        spans = [(sum(PIECES[:i]), PIECES[i]) for i in range(len(PIECES))]
-        early = spans[-1][0]
+        spans = [[(sum(widths[:i]), widths[i]) for i in range(len(widths))] for widths in PIECES]
+        early = S
         early_codes = keep.tile([P, early], U16, name="early_codes", align_bytes=64)
-        for first, width in spans[:-1]:
+        for first, width in spans[0]:
             gather_words(0, first, width, early_codes[:, first : first + width])
 
         w_bf = keep.tile([P, PASSES, M, PACK], BF16, name="w_bf", align_bytes=64)
@@ -126,9 +127,9 @@ def tile_picked_median_gelu_p_kernel(
                     nc.scalar.activation(y[:, g * GROUP : (g + 1) * GROUP], banks[g][:], GELU)
 
         late_codes = keep.tile([P, PASSES * S - early], U16, name="late_codes", tag="w_raw1", align_bytes=64)
-        for first, width in spans[:-1]:
+        for first, width in spans[0]:
             multiply(0, first, width, early_codes[:, first : first + width])
-        for z, first, width in [(0,) + spans[-1]] + [(1,) + span for span in spans]:
+        for z, first, width in [(1,) + span for span in spans[1]]:
             at = z * S + first - early
             gather_words(z, first, width, late_codes[:, at : at + width])
             multiply(z, first, width, late_codes[:, at : at + width])

@@ -18,21 +18,22 @@ MAX = mybir.AluOpType.max
 MIN = mybir.AluOpType.min
 ADD = mybir.AluOpType.add
 SUB = mybir.AluOpType.subtract
+MULT = mybir.AluOpType.mult
 RELU = mybir.ActivationFunctionType.Relu
 COPY = mybir.ActivationFunctionType.Copy
-MULT = mybir.AluOpType.mult
 GELU = mybir.ActivationFunctionType.Gelu_apprx_tanh
 
 P = 128
 PACK = 4
 PASSES = K // (P * PACK)
-BLOCKS = 16
+SCALE_ROWS = 16
 QUADRANT = 32
-QUADRANT_ROWS = BLOCKS * QUADRANT // P
+QUADRANT_ROWS = SCALE_ROWS * QUADRANT // P
 STRIPE = 16
+RUN = 4
 GROUP = 128
-PIECES = ((1024,), (384, 384, 256))
-BOUND_BLOCKS = 3
+PIECES = (384, 384, 256)
+SQUARES = 3
 
 
 def tile_picked_median_gelu_p_kernel(
@@ -43,22 +44,21 @@ def tile_picked_median_gelu_p_kernel(
         keep = ctx.enter_context(tc.tile_pool(name="keep", bufs=1))
         psum = ctx.enter_context(tc.psum_pool(name="psum", bufs=1))
 
-        scale_rows = PASSES * BLOCKS
+        first_row = P - PASSES * SCALE_ROWS
         scale_table = keep.tile([P, T], U8, name="scale_table", align_bytes=64)
         nc.sync.dma_start(
-            scale_table[P - scale_rows : P, :].bitcast(I32),
+            scale_table[first_row:P, :].bitcast(I32),
             x_scales.rearrange("z q c -> (z q) c").bitcast(I32),
         )
         offs_sb = keep.tile([P, S // STRIPE], U16, name="offs_sb")
         nc.sync.dma_start(offs_sb[:], offs)
-        nc.vector.memset(scale_table[0 : P - scale_rows, :].bitcast(I32), 0)
+        nc.vector.memset(scale_table[0:first_row, :].bitcast(I32), 0)
 
-        word_table = [keep.tile([P, w], U16, name=f"word_table{z}", align_bytes=64) for z, w in enumerate((2 * T, T))]
+        word_table = [
+            keep.tile([P, width], U16, name=f"word_table{z}", align_bytes=64) for z, width in enumerate((2 * T, T))
+        ]
         nc.vector.memset(word_table[0][:, T:].bitcast(I32), 0)
         w_raw = [keep.tile([P, PACK, M], F32, name=f"w_raw{z}", tag=f"w_raw{z}", align_bytes=64) for z in range(PASSES)]
-        warm = keep.tile([P, 2], F32, name="warm")
-        nc.vector.memset(warm[:, 0:1], 0.0)
-        nc.scalar.activation(warm[:, 1:2], warm[:, 0:1], GELU)
         pos_sb = []
         for d, pos in enumerate((pos1, pos2, pos3)):
             pos_tile = keep.tile([P, V // STRIPE], U16, name=f"pos_sb{d}")
@@ -80,30 +80,23 @@ def tile_picked_median_gelu_p_kernel(
         nc.vector.tensor_copy(picked_scales[:], scale_table[:].indirect(offs_sb[:]))
         for z in range(PASSES):
             for q in range(P // QUADRANT):
-                row = P - scale_rows + BLOCKS * z + QUADRANT_ROWS * q
+                row = first_row + SCALE_ROWS * z + QUADRANT_ROWS * q
                 nc.sync.dma_start(
                     x_plane[z][QUADRANT * q : QUADRANT * q + QUADRANT_ROWS, :].bitcast(I32),
                     picked_scales[row : row + QUADRANT_ROWS, :].bitcast(I32),
                 )
 
-        def gather_words(z, first, width, codes):
-            nc.vector.tensor_copy(
-                codes, word_table[z][:].indirect(offs_sb[:, first // STRIPE : (first + width) // STRIPE])
-            )
-
         banks = [psum.tile([M, GROUP], F32, name=f"bank{g}", tag=f"bank{g}") for g in range(S // GROUP)]
         y = keep.tile([P, S], F32, name="y")
 
-        spans = [[(sum(widths[:i]), widths[i]) for i in range(len(widths))] for widths in PIECES]
-        early = S
-        early_codes = keep.tile([P, early], U16, name="early_codes", align_bytes=64)
-        for first, width in spans[0]:
-            gather_words(0, first, width, early_codes[:, first : first + width])
+        codes0 = keep.tile([P, S], U16, name="codes0", align_bytes=64)
+        nc.vector.tensor_copy(codes0[:], word_table[0][:].indirect(offs_sb[:]))
 
         w_bf = keep.tile([P, PASSES, M, PACK], BF16, name="w_bf", align_bytes=64)
         for z in range(PASSES):
             nc.scalar.copy(
-                w_bf[:, z].rearrange("p (c i) j -> p c j i", i=4), w_raw[z][:].rearrange("p j (c i) -> p c j i", i=4)
+                w_bf[:, z].rearrange("p (c i) j -> p c j i", i=RUN),
+                w_raw[z][:].rearrange("p j (c i) -> p c j i", i=RUN),
             )
         w_codes = keep.tile([P, PASSES * M], U32, name="w_codes", align_bytes=64)
         w_plane = keep.tile([P, PASSES * M], U8, name="w_plane", align_bytes=64)
@@ -111,98 +104,102 @@ def tile_picked_median_gelu_p_kernel(
             out=w_codes[:].bitcast(FP8X4), scales=w_plane[:], in_=w_bf[:].rearrange("p z m j -> p (z m j)")
         )
 
-        def multiply(z, first, width, codes):
-            for c in range(0, width, GROUP):
-                g = (first + c) // GROUP
-                nc.tensor.matmul_mx(
-                    out=banks[g][:],
-                    lhsT=w_codes[:, z * M : (z + 1) * M].bitcast(FP8X4),
-                    lhsT_scale=w_plane[:, z * M : (z + 1) * M],
-                    rhs=codes[:, c : c + GROUP].bitcast(FP4X4),
-                    rhs_scale=x_plane[z][:, first + c : first + c + GROUP],
-                    start=(z == 0),
-                    stop=(z == PASSES - 1),
-                )
-                if z == PASSES - 1:
-                    nc.scalar.activation(y[:, g * GROUP : (g + 1) * GROUP], banks[g][:], GELU)
+        def multiply(z, codes, g):
+            columns = slice(g * GROUP, (g + 1) * GROUP)
+            nc.tensor.matmul_mx(
+                out=banks[g][:],
+                lhsT=w_codes[:, z * M : (z + 1) * M].bitcast(FP8X4),
+                lhsT_scale=w_plane[:, z * M : (z + 1) * M],
+                rhs=codes[:, columns].bitcast(FP4X4),
+                rhs_scale=x_plane[z][:, columns],
+                start=(z == 0),
+                stop=(z == PASSES - 1),
+            )
 
-        late_codes = keep.tile([P, PASSES * S - early], U16, name="late_codes", tag="w_raw1", align_bytes=64)
-        for first, width in spans[0]:
-            multiply(0, first, width, early_codes[:, first : first + width])
-        for z, first, width in [(1,) + span for span in spans[1]]:
-            at = z * S + first - early
-            gather_words(z, first, width, late_codes[:, at : at + width])
-            multiply(z, first, width, late_codes[:, at : at + width])
+        codes1 = keep.tile([P, S], U16, name="codes1", tag="w_raw1", align_bytes=64)
+        for g in range(S // GROUP):
+            multiply(0, codes0, g)
+        for i, width in enumerate(PIECES):
+            begin = sum(PIECES[:i])
+            end = begin + width
+            nc.vector.tensor_copy(
+                codes1[:, begin:end], word_table[1][:].indirect(offs_sb[:, begin // STRIPE : end // STRIPE])
+            )
+            for g in range(begin // GROUP, end // GROUP):
+                multiply(1, codes1, g)
+                nc.scalar.activation(y[:, g * GROUP : (g + 1) * GROUP], banks[g][:], GELU)
 
-        def entries(d, a, b):
-            return y[:].indirect(pos_sb[d][:, a // STRIPE : b // STRIPE])
+        def neighbours(d, begin, end):
+            return y[:].indirect(pos_sb[d][:, begin // STRIPE : end // STRIPE])
 
-        def turn(bank, block, start, stop):
-            nc.tensor.matmul(bank, lhsT=block, rhs=ident[:], is_transpose=True, start=start, stop=stop)
+        def turn(bank, square, start, stop):
+            nc.tensor.matmul(bank, lhsT=square, rhs=ident[:], is_transpose=True, start=start, stop=stop)
 
-        first = BOUND_BLOCKS * P
-        rest = V - first
-        last_block = BOUND_BLOCKS - 1
-        blocks = [slice(j * P, (j + 1) * P) for j in range(BOUND_BLOCKS)]
-        a_spans = [(0, last_block), (last_block, BOUND_BLOCKS)]
-        mid = V // 2
-        a_half = [keep.tile([P, mid], F32, name=f"a_half{i}", tag=f"a_first{i}") for i in range(2)]
-        a_first = [a_half[0][:], a_half[1][:, : first - mid]]
-        a_rest = a_half[1][:, first - mid :]
-        d1_half = [keep.tile([P, mid], F32, name=f"d1_half{i}", tag=f"d1_first{i}") for i in range(2)]
-        d1_first = [d1_half[0][:], d1_half[1][:, : first - mid]]
-        d1_rest = d1_half[1][:, first - mid :]
-        d2_rest = keep.tile([P, rest], F32, name="d2_rest", tag="d2_rest")
+        bounded = SQUARES * P
+        plain = V - bounded
+        half = V // 2
+        squares = [slice(j * P, (j + 1) * P) for j in range(SQUARES)]
+        squares_of = [range(0, half // P), range(half // P, SQUARES)]
+        a_half = [keep.tile([P, half], F32, name=f"a_half{i}", tag=f"a_half{i}") for i in range(2)]
+        d1_half = [keep.tile([P, half], F32, name=f"d1_half{i}", tag=f"d1_half{i}") for i in range(2)]
+        a_plain = a_half[1][:, bounded - half :]
+        d1_plain = d1_half[1][:, bounded - half :]
+        d2_plain = keep.tile([P, plain], F32, name="d2_plain", tag="d2_plain")
         for i in range(2):
-            nc.vector.tensor_copy(a_half[i][:], entries(0, i * mid, (i + 1) * mid))
+            nc.vector.tensor_copy(a_half[i][:], neighbours(0, i * half, (i + 1) * half))
         for i in range(2):
-            nc.vector.tensor_tensor(d1_half[i][:], entries(1, i * mid, (i + 1) * mid), a_half[i][:], SUB)
-        nc.vector.tensor_tensor(d2_rest[:], entries(2, first, V), a_rest, SUB)
+            nc.vector.tensor_tensor(d1_half[i][:], neighbours(1, i * half, (i + 1) * half), a_half[i][:], SUB)
+        nc.vector.tensor_tensor(d2_plain[:], neighbours(2, bounded, V), a_plain, SUB)
 
-        a_bank = [psum.tile([P, (e - b) * P], F32, name=f"a_bank{i}", tag=f"bank{i}") for i, (b, e) in enumerate(a_spans)]
-        d_bank = [psum.tile([P, P], F32, name=f"d_bank{j}", tag=f"bank{2 + j}") for j in range(BOUND_BLOCKS)]
-        high = [psum.tile([P, P], F32, name=f"high{j}", tag=f"bank{5 + j}") for j in range(BOUND_BLOCKS)]
-        low = [psum.tile([P, P], F32, name=f"low{j}", tag=f"bank{j}") for j in range(BOUND_BLOCKS)]
-        a_t = keep.tile([P, first], F32, name="a_t")
-        minus_a_t = keep.tile([P, first], F32, name="minus_a_t")
-        up_t = keep.tile([P, first], F32, name="up_t", tag="up_t")
-        down_t = keep.tile([P, first], F32, name="down_t", tag="down_t")
-        for i, (b, e) in enumerate(a_spans):
-            for j in range(b, e):
-                turn(a_bank[i][:, blocks[j - b]], a_first[i][:, blocks[j - b]], True, True)
-            nc.scalar.copy(a_t[:, b * P : e * P], a_bank[i][:])
-        for i, (b, e) in enumerate(a_spans):
-            nc.scalar.activation(minus_a_t[:, b * P : e * P], a_bank[i][:], COPY, scale=-1.0)
-        for j, s in enumerate(blocks):
+        a_bank = [psum.tile([P, len(squares_of[i]) * P], F32, name=f"a_bank{i}", tag=f"bank{i}") for i in range(2)]
+        d1_bank = [psum.tile([P, P], F32, name=f"d1_bank{j}", tag=f"bank{2 + j}") for j in range(SQUARES)]
+        high = [psum.tile([P, P], F32, name=f"high{j}", tag=f"bank{2 + SQUARES + j}") for j in range(SQUARES)]
+        minus_low = [psum.tile([P, P], F32, name=f"minus_low{j}", tag=f"bank{j}") for j in range(SQUARES)]
+        a_t = keep.tile([P, bounded], F32, name="a_t")
+        minus_a_t = keep.tile([P, bounded], F32, name="minus_a_t")
+        up_t = keep.tile([P, bounded], F32, name="up_t")
+        down_t = keep.tile([P, bounded], F32, name="down_t")
+        span_of = [slice(js.start * P, js.stop * P) for js in squares_of]
+        for i in range(2):
+            for s in squares[: len(squares_of[i])]:
+                turn(a_bank[i][:, s], a_half[i][:, s], True, True)
+            nc.scalar.copy(a_t[:, span_of[i]], a_bank[i][:])
+        for i in range(2):
+            nc.scalar.activation(minus_a_t[:, span_of[i]], a_bank[i][:], COPY, scale=-1.0)
+        for j, s in enumerate(squares):
             turn(high[j][:], a_t[:, s], True, False)
-        for i, (b, e) in enumerate(a_spans):
-            for j in range(b, e):
-                turn(d_bank[j][:], d1_first[i][:, blocks[j - b]], True, True)
-        for j, s in enumerate(blocks):
-            nc.scalar.activation(up_t[:, s], d_bank[j][:], RELU)
-        for j, s in enumerate(blocks):
+        for i in range(2):
+            for j, s in zip(squares_of[i], squares):
+                turn(d1_bank[j][:], d1_half[i][:, s], True, True)
+        for j, s in enumerate(squares):
+            nc.scalar.activation(up_t[:, s], d1_bank[j][:], RELU)
+        for j, s in enumerate(squares):
             turn(high[j][:], up_t[:, s], False, True)
-        for j, s in enumerate(blocks):
-            nc.scalar.activation(down_t[:, s], d_bank[j][:], RELU, scale=-1.0)
-        for j, s in enumerate(blocks):
-            turn(low[j][:], minus_a_t[:, s], True, False)
-            turn(low[j][:], down_t[:, s], False, True)
+        for j, s in enumerate(squares):
+            nc.scalar.activation(down_t[:, s], d1_bank[j][:], RELU, scale=-1.0)
+        for j, s in enumerate(squares):
+            turn(minus_low[j][:], minus_a_t[:, s], True, False)
+            turn(minus_low[j][:], down_t[:, s], False, True)
 
-        c_block = [keep.tile([P, P], F32, name=f"c_block{j}", tag=tag) for j, tag in enumerate(("a_first0", "d1_first0", "d2_rest"))]
-        cut = keep.tile([P, rest], F32, name="cut")
-        shift = keep.tile([P, rest], F32, name="shift")
-        capped = keep.tile([P, first], F32, name="capped")
-        nc.vector.tensor_copy(c_block[0][:], entries(2, 0, P))
-        nc.vector.scalar_tensor_tensor(cut[:], d1_rest, 0.0, d2_rest[:], MAX, MIN)
-        nc.vector.tensor_copy(c_block[1][:], entries(2, P, 2 * P))
-        nc.vector.scalar_tensor_tensor(shift[:], d1_rest, 0.0, cut[:], MIN, MAX)
-        nc.vector.tensor_copy(c_block[2][:], entries(2, 2 * P, first))
-        for s, c, bound in zip(blocks, c_block, high):
-            nc.vector.tensor_tensor(capped[:, s], bound[:], c[:], MIN)
-        med_rest = keep.tile([P, rest], F32, name="med_rest")
-        nc.gpsimd.tensor_tensor(med_rest[:], shift[:], a_rest, ADD)
-        nc.sync.dma_start(out[:, first:], med_rest[:])
-        for j, s in enumerate(blocks):
-            med = keep.tile([P, P], F32, name=f"med{j}")
-            nc.vector.scalar_tensor_tensor(med[:], low[j][:], -1.0, capped[:, s], MULT, MAX)
-            nc.sync.dma_start(out[:, s], med[:])
+        c = [
+            keep.tile([P, P], F32, name=f"c{j}", tag=tag) for j, tag in enumerate(("a_half0", "d1_half0", "d2_plain"))
+        ]
+        cut = keep.tile([P, plain], F32, name="cut")
+        shift = keep.tile([P, plain], F32, name="shift")
+        capped = keep.tile([P, bounded], F32, name="capped")
+        nc.vector.tensor_copy(c[0][:], neighbours(2, 0, P))
+        nc.vector.scalar_tensor_tensor(cut[:], d1_plain, 0.0, d2_plain[:], MAX, MIN)
+        nc.vector.tensor_copy(c[1][:], neighbours(2, P, 2 * P))
+        nc.vector.scalar_tensor_tensor(shift[:], d1_plain, 0.0, cut[:], MIN, MAX)
+        nc.vector.tensor_copy(c[2][:], neighbours(2, 2 * P, bounded))
+        for j, s in enumerate(squares):
+            nc.vector.tensor_tensor(capped[:, s], high[j][:], c[j][:], MIN)
+
+        median_plain = keep.tile([P, plain], F32, name="median_plain")
+        nc.gpsimd.tensor_tensor(median_plain[:], shift[:], a_plain, ADD)
+        nc.sync.dma_start(out[:, bounded:], median_plain[:])
+
+        for j, s in enumerate(squares):
+            median = keep.tile([P, P], F32, name=f"median{j}")
+            nc.vector.scalar_tensor_tensor(median[:], minus_low[j][:], -1.0, capped[:, s], MULT, MAX)
+            nc.sync.dma_start(out[:, s], median[:])

@@ -57,7 +57,6 @@ def tile_picked_median_gelu_p_kernel(
         word_table = [
             keep.tile([P, width], U16, name=f"word_table{z}", align_bytes=64) for z, width in enumerate((2 * T, T))
         ]
-        nc.vector.memset(word_table[0][:, T:].bitcast(I32), 0)
         w_raw = [keep.tile([P, PACK, M], F32, name=f"w_raw{z}", tag=f"w_raw{z}", align_bytes=64) for z in range(PASSES)]
         pos_sb = []
         for d, pos in enumerate((pos1, pos2, pos3)):

@@ -41,26 +41,30 @@ def tile_picked_median_gelu_p_kernel(
 ):
     nc = tc.nc
     with ExitStack() as ctx:
+        tables = ctx.enter_context(tc.tile_pool(name="tables", bufs=1))
+        first_gap = ctx.enter_context(tc.tile_pool(name="first_gap", bufs=1))
+        lists = ctx.enter_context(tc.tile_pool(name="lists", bufs=1))
+        second_gap = ctx.enter_context(tc.tile_pool(name="second_gap", bufs=1))
         keep = ctx.enter_context(tc.tile_pool(name="keep", bufs=1))
         psum = ctx.enter_context(tc.psum_pool(name="psum", bufs=1))
 
         first_row = P - PASSES * SCALE_ROWS
-        scale_table = keep.tile([P, T], U8, name="scale_table", align_bytes=64)
+        scale_table = tables.tile([P, T], U8, name="scale_table", align_bytes=256)
         nc.sync.dma_start(
             scale_table[first_row:P, :].bitcast(I32),
             x_scales.rearrange("z q c -> (z q) c").bitcast(I32),
         )
-        offs_sb = keep.tile([P, S // STRIPE], U16, name="offs_sb")
+        offs_sb = lists.tile([P, S // STRIPE], U16, name="offs_sb")
         nc.sync.dma_start(offs_sb[:], offs)
         nc.vector.memset(scale_table[0:first_row, :].bitcast(I32), 0)
 
         word_table = [
-            keep.tile([P, width], U16, name=f"word_table{z}", align_bytes=64) for z, width in enumerate((2 * T, T))
+            tables.tile([P, width], U16, name=f"word_table{z}", align_bytes=256) for z, width in enumerate((2 * T, T))
         ]
         w_raw = [keep.tile([P, PACK, M], F32, name=f"w_raw{z}", tag=f"w_raw{z}", align_bytes=64) for z in range(PASSES)]
         pos_sb = []
         for d, pos in enumerate((pos1, pos2, pos3)):
-            pos_tile = keep.tile([P, V // STRIPE], U16, name=f"pos_sb{d}")
+            pos_tile = lists.tile([P, V // STRIPE], U16, name=f"pos_sb{d}")
             nc.sync.dma_start(pos_tile[:], pos)
             pos_sb.append(pos_tile)
         nc.sync.dma_start(word_table[0][:, :T].bitcast(I32), x_words[0].bitcast(I32))
@@ -68,10 +72,10 @@ def tile_picked_median_gelu_p_kernel(
             nc.sync.dma_start(w_raw[z][:], w1.rearrange("(z p j) m -> z p j m", z=PASSES, j=PACK)[z])
         nc.sync.dma_start(word_table[1][:].bitcast(I32), x_words[1].bitcast(I32))
 
-        ident = keep.tile([P, P], F32, name="ident")
+        ident = first_gap.tile([P, P], F32, name="ident", offset=48 * 1024)
         make_identity(nc, ident[:])
 
-        x_planes = keep.tile([P, PASSES * S], U8, name="x_planes", align_bytes=64)
+        x_planes = second_gap.tile([P, PASSES * S], U8, name="x_planes", align_bytes=64, offset=64 * 1024)
         nc.vector.memset(x_planes[:].bitcast(I32), 0)
         x_plane = [x_planes[:, z * S : (z + 1) * S] for z in range(PASSES)]
 
@@ -86,7 +90,7 @@ def tile_picked_median_gelu_p_kernel(
                 )
 
         banks = [psum.tile([M, GROUP], F32, name=f"bank{g}", tag=f"bank{g}") for g in range(S // GROUP)]
-        y = keep.tile([P, S], F32, name="y")
+        y = tables.tile([P, S], F32, name="y", align_bytes=256)
 
         codes0 = keep.tile([P, S], U16, name="codes0", align_bytes=64)
         nc.vector.tensor_copy(codes0[:], word_table[0][:].indirect(offs_sb[:]))

@@ -34,6 +34,8 @@ RUN = 4
 GROUP = 128
 PIECES = (384, 384, 256)
 SQUARES = 3
+GAP_TO_LISTS = 48 * 1024
+GAP_TO_OTHERS = 64 * 1024
 
 
 def tile_picked_median_gelu_p_kernel(
@@ -72,10 +74,10 @@ def tile_picked_median_gelu_p_kernel(
             nc.sync.dma_start(w_raw[z][:], w1.rearrange("(z p j) m -> z p j m", z=PASSES, j=PACK)[z])
         nc.sync.dma_start(word_table[1][:].bitcast(I32), x_words[1].bitcast(I32))
 
-        ident = first_gap.tile([P, P], F32, name="ident", offset=48 * 1024)
+        ident = first_gap.tile([P, P], F32, name="ident", offset=GAP_TO_LISTS)
         make_identity(nc, ident[:])
 
-        x_planes = second_gap.tile([P, PASSES * S], U8, name="x_planes", align_bytes=64, offset=64 * 1024)
+        x_planes = second_gap.tile([P, PASSES * S], U8, name="x_planes", align_bytes=64, offset=GAP_TO_OTHERS)
         nc.vector.memset(x_planes[:].bitcast(I32), 0)
         x_plane = [x_planes[:, z * S : (z + 1) * S] for z in range(PASSES)]
 
@@ -148,11 +150,14 @@ def tile_picked_median_gelu_p_kernel(
         a_plain = a_half[1][:, bounded - half :]
         d1_plain = d1_half[1][:, bounded - half :]
         d2_plain = keep.tile([P, plain], F32, name="d2_plain", tag="d2_plain")
-        for i in range(2):
-            nc.vector.tensor_copy(a_half[i][:], neighbours(0, i * half, (i + 1) * half))
-        for i in range(2):
-            nc.vector.tensor_tensor(d1_half[i][:], neighbours(1, i * half, (i + 1) * half), a_half[i][:], SUB)
-        nc.vector.tensor_tensor(d2_plain[:], neighbours(2, bounded, V), a_plain, SUB)
+        half_begin = (half, 0)
+        square_begin = (half, half + P, 0)
+        plain_begin = P
+        for i, begin in enumerate(half_begin):
+            nc.vector.tensor_copy(a_half[i][:], neighbours(0, begin, begin + half))
+        for i, begin in enumerate(half_begin):
+            nc.vector.tensor_tensor(d1_half[i][:], neighbours(1, begin, begin + half), a_half[i][:], SUB)
+        nc.vector.tensor_tensor(d2_plain[:], neighbours(2, plain_begin, plain_begin + plain), a_plain, SUB)
 
         a_bank = [psum.tile([P, len(squares_of[i]) * P], F32, name=f"a_bank{i}", tag=f"bank{i}") for i in range(2)]
         d1_bank = [psum.tile([P, P], F32, name=f"d1_bank{j}", tag=f"bank{2 + j}") for j in range(SQUARES)]
@@ -190,19 +195,21 @@ def tile_picked_median_gelu_p_kernel(
         cut = keep.tile([P, plain], F32, name="cut")
         shift = keep.tile([P, plain], F32, name="shift")
         capped = keep.tile([P, bounded], F32, name="capped")
-        nc.vector.tensor_copy(c[0][:], neighbours(2, 0, P))
+        nc.vector.tensor_copy(c[0][:], neighbours(2, square_begin[0], square_begin[0] + P))
         nc.vector.scalar_tensor_tensor(cut[:], d1_plain, 0.0, d2_plain[:], MAX, MIN)
-        nc.vector.tensor_copy(c[1][:], neighbours(2, P, 2 * P))
+        nc.vector.tensor_copy(c[1][:], neighbours(2, square_begin[1], square_begin[1] + P))
         nc.vector.scalar_tensor_tensor(shift[:], d1_plain, 0.0, cut[:], MIN, MAX)
-        nc.vector.tensor_copy(c[2][:], neighbours(2, 2 * P, bounded))
+        nc.vector.tensor_copy(c[2][:], neighbours(2, square_begin[2], square_begin[2] + P))
         for j, s in enumerate(squares):
             nc.vector.tensor_tensor(capped[:, s], high[j][:], c[j][:], MIN)
 
-        median_plain = keep.tile([P, plain], F32, name="median_plain")
-        nc.gpsimd.tensor_tensor(median_plain[:], shift[:], a_plain, ADD)
-        nc.sync.dma_start(out[:, bounded:], median_plain[:])
+        median = keep.tile([P, V], F32, name="median", align_bytes=256)
+        nc.gpsimd.tensor_tensor(median[:, plain_begin : plain_begin + plain], shift[:], a_plain, ADD)
 
+        store_begin = (plain_begin,) + square_begin[1:]
         for j, s in enumerate(squares):
-            median = keep.tile([P, P], F32, name=f"median{j}")
-            nc.vector.scalar_tensor_tensor(median[:], minus_low[j][:], -1.0, capped[:, s], MULT, MAX)
-            nc.sync.dma_start(out[:, s], median[:])
+            end = square_begin[j] + P
+            nc.vector.scalar_tensor_tensor(
+                median[:, square_begin[j] : end], minus_low[j][:], -1.0, capped[:, s], MULT, MAX
+            )
+            nc.sync.dma_start(out[:, store_begin[j] : end], median[:, store_begin[j] : end])

@@ -1,7 +1,6 @@
 from contextlib import ExitStack
 
 import concourse.mybir as mybir
-from concourse.masks import make_identity
 
 K, T, S, V, M = 1024, 2048, 1024, 512, 128
 FLOPS = 2 * K * M * S
@@ -18,8 +17,6 @@ MAX = mybir.AluOpType.max
 MIN = mybir.AluOpType.min
 ADD = mybir.AluOpType.add
 SUB = mybir.AluOpType.subtract
-MULT = mybir.AluOpType.mult
-RELU = mybir.ActivationFunctionType.Relu
 COPY = mybir.ActivationFunctionType.Copy
 GELU = mybir.ActivationFunctionType.Gelu_apprx_tanh
 
@@ -33,7 +30,7 @@ STRIPE = 16
 RUN = 4
 GROUP = 128
 PIECES = (384, 384, 256)
-SQUARES = 3
+CHUNK = 128
 GAP_TO_LISTS = 48 * 1024
 GAP_TO_OTHERS = 64 * 1024
 
@@ -74,9 +71,7 @@ def tile_picked_median_gelu_p_kernel(
             nc.sync.dma_start(w_raw[z][:], w1.rearrange("(z p j) m -> z p j m", z=PASSES, j=PACK)[z])
         nc.sync.dma_start(word_table[1][:].bitcast(I32), x_words[1].bitcast(I32))
 
-        ident = first_gap.tile([P, P], F32, name="ident", offset=GAP_TO_LISTS)
-        make_identity(nc, ident[:])
-
+        w_bf = first_gap.tile([P, PASSES, M, PACK], BF16, name="w_bf", align_bytes=64, offset=GAP_TO_LISTS)
         x_planes = second_gap.tile([P, PASSES * S], U8, name="x_planes", align_bytes=64, offset=GAP_TO_OTHERS)
         nc.vector.memset(x_planes[:].bitcast(I32), 0)
         x_plane = [x_planes[:, z * S : (z + 1) * S] for z in range(PASSES)]
@@ -97,7 +92,6 @@ def tile_picked_median_gelu_p_kernel(
         codes0 = keep.tile([P, S], U16, name="codes0", align_bytes=64)
         nc.vector.tensor_copy(codes0[:], word_table[0][:].indirect(offs_sb[:]))
 
-        w_bf = keep.tile([P, PASSES, M, PACK], BF16, name="w_bf", align_bytes=64)
         for z in range(PASSES):
             nc.scalar.copy(
                 w_bf[:, z].rearrange("p (c i) j -> p c j i", i=RUN),
@@ -134,82 +128,59 @@ def tile_picked_median_gelu_p_kernel(
                 multiply(1, codes1, g)
                 nc.scalar.activation(y[:, g * GROUP : (g + 1) * GROUP], banks[g][:], GELU)
 
-        def neighbours(d, begin, end):
-            return y[:].indirect(pos_sb[d][:, begin // STRIPE : end // STRIPE])
+        def neighbours(d, j):
+            return y[:].indirect(pos_sb[d][:, j * CHUNK // STRIPE : (j + 1) * CHUNK // STRIPE])
 
-        def turn(bank, square, start, stop):
-            nc.tensor.matmul(bank, lhsT=square, rhs=ident[:], is_transpose=True, start=start, stop=stop)
+        def square(name):
+            return keep.tile([P, CHUNK], F32, name=name, tag=name, align_bytes=64)
 
-        bounded = SQUARES * P
-        plain = V - bounded
-        half = V // 2
-        squares = [slice(j * P, (j + 1) * P) for j in range(SQUARES)]
-        squares_of = [range(0, half // P), range(half // P, SQUARES)]
-        a_half = [keep.tile([P, half], F32, name=f"a_half{i}", tag=f"a_half{i}") for i in range(2)]
-        d1_half = [keep.tile([P, half], F32, name=f"d1_half{i}", tag=f"d1_half{i}") for i in range(2)]
-        a_plain = a_half[1][:, bounded - half :]
-        d1_plain = d1_half[1][:, bounded - half :]
-        d2_plain = keep.tile([P, plain], F32, name="d2_plain", tag="d2_plain")
-        half_begin = (half, 0)
-        square_begin = (half, half + P, 0)
-        plain_begin = P
-        for i, begin in enumerate(half_begin):
-            nc.vector.tensor_copy(a_half[i][:], neighbours(0, begin, begin + half))
-        for i, begin in enumerate(half_begin):
-            nc.vector.tensor_tensor(d1_half[i][:], neighbours(1, begin, begin + half), a_half[i][:], SUB)
-        nc.vector.tensor_tensor(d2_plain[:], neighbours(2, plain_begin, plain_begin + plain), a_plain, SUB)
-
-        a_bank = [psum.tile([P, len(squares_of[i]) * P], F32, name=f"a_bank{i}", tag=f"bank{i}") for i in range(2)]
-        d1_bank = [psum.tile([P, P], F32, name=f"d1_bank{j}", tag=f"bank{2 + j}") for j in range(SQUARES)]
-        high = [psum.tile([P, P], F32, name=f"high{j}", tag=f"bank{2 + SQUARES + j}") for j in range(SQUARES)]
-        minus_low = [psum.tile([P, P], F32, name=f"minus_low{j}", tag=f"bank{j}") for j in range(SQUARES)]
-        a_t = keep.tile([P, bounded], F32, name="a_t")
-        minus_a_t = keep.tile([P, bounded], F32, name="minus_a_t")
-        up_t = keep.tile([P, bounded], F32, name="up_t")
-        down_t = keep.tile([P, bounded], F32, name="down_t")
-        span_of = [slice(js.start * P, js.stop * P) for js in squares_of]
-        for i in range(2):
-            for s in squares[: len(squares_of[i])]:
-                turn(a_bank[i][:, s], a_half[i][:, s], True, True)
-            nc.scalar.copy(a_t[:, span_of[i]], a_bank[i][:])
-        for i in range(2):
-            nc.scalar.activation(minus_a_t[:, span_of[i]], a_bank[i][:], COPY, scale=-1.0)
-        for j, s in enumerate(squares):
-            turn(high[j][:], a_t[:, s], True, False)
-        for i in range(2):
-            for j, s in zip(squares_of[i], squares):
-                turn(d1_bank[j][:], d1_half[i][:, s], True, True)
-        for j, s in enumerate(squares):
-            nc.scalar.activation(up_t[:, s], d1_bank[j][:], RELU)
-        for j, s in enumerate(squares):
-            turn(high[j][:], up_t[:, s], False, True)
-        for j, s in enumerate(squares):
-            nc.scalar.activation(down_t[:, s], d1_bank[j][:], RELU, scale=-1.0)
-        for j, s in enumerate(squares):
-            turn(minus_low[j][:], minus_a_t[:, s], True, False)
-            turn(minus_low[j][:], down_t[:, s], False, True)
-
-        c = [
-            keep.tile([P, P], F32, name=f"c{j}", tag=tag) for j, tag in enumerate(("a_half0", "d1_half0", "d2_plain"))
-        ]
-        cut = keep.tile([P, plain], F32, name="cut")
-        shift = keep.tile([P, plain], F32, name="shift")
-        capped = keep.tile([P, bounded], F32, name="capped")
-        nc.vector.tensor_copy(c[0][:], neighbours(2, square_begin[0], square_begin[0] + P))
-        nc.vector.scalar_tensor_tensor(cut[:], d1_plain, 0.0, d2_plain[:], MAX, MIN)
-        nc.vector.tensor_copy(c[1][:], neighbours(2, square_begin[1], square_begin[1] + P))
-        nc.vector.scalar_tensor_tensor(shift[:], d1_plain, 0.0, cut[:], MIN, MAX)
-        nc.vector.tensor_copy(c[2][:], neighbours(2, square_begin[2], square_begin[2] + P))
-        for j, s in enumerate(squares):
-            nc.vector.tensor_tensor(capped[:, s], high[j][:], c[j][:], MIN)
-
+        chunks = V // CHUNK
+        a = [square(f"a{j}") for j in range(chunks)]
+        b = [square(f"b{j}") for j in range(chunks)]
+        c = [square(f"c{j}") for j in range(chunks)]
+        high = [square(f"high{j}") for j in range(chunks)]
+        low = [square(f"low{j}") for j in range(chunks)]
+        capped = [square(f"capped{j}") for j in range(chunks)]
         median = keep.tile([P, V], F32, name="median", align_bytes=256)
-        nc.gpsimd.tensor_tensor(median[:, plain_begin : plain_begin + plain], shift[:], a_plain, ADD)
 
-        store_begin = (plain_begin,) + square_begin[1:]
-        for j, s in enumerate(squares):
-            end = square_begin[j] + P
-            nc.vector.scalar_tensor_tensor(
-                median[:, square_begin[j] : end], minus_low[j][:], -1.0, capped[:, s], MULT, MAX
-            )
-            nc.sync.dma_start(out[:, store_begin[j] : end], median[:, store_begin[j] : end])
+        def fetch(tile, d, j):
+            nc.scalar.activation(tile[j][:], neighbours(d, j), COPY)
+
+        def bounds(j):
+            nc.vector.tensor_tensor(high[j][:], a[j][:], b[j][:], MAX)
+            nc.vector.tensor_tensor(low[j][:], a[j][:], b[j][:], MIN)
+
+        def cap(j):
+            nc.vector.tensor_tensor(capped[j][:], high[j][:], c[j][:], MIN)
+
+        def finish(j):
+            columns = slice(j * CHUNK, (j + 1) * CHUNK)
+            nc.vector.tensor_tensor(median[:, columns], low[j][:], capped[j][:], MAX)
+            nc.sync.dma_start(out[:, columns], median[:, columns])
+
+        fetch(a, 0, 0)
+        fetch(a, 0, 1)
+        fetch(c, 2, 1)
+        for j in (2, 3):
+            fetch(a, 0, j)
+            fetch(b, 1, j)
+        for j in (2, 3):
+            fetch(c, 2, j)
+
+        nc.vector.tensor_copy(b[1][:], neighbours(1, 1))
+        nc.vector.tensor_tensor(b[0][:], neighbours(1, 0), a[0][:], SUB)
+        nc.vector.tensor_tensor(c[0][:], neighbours(2, 0), a[0][:], SUB)
+        nc.vector.tensor_tensor(high[1][:], a[1][:], b[1][:], MAX)
+        nc.vector.scalar_tensor_tensor(high[0][:], b[0][:], 0.0, c[0][:], MAX, MIN)
+        nc.vector.tensor_tensor(low[1][:], a[1][:], b[1][:], MIN)
+        nc.vector.scalar_tensor_tensor(low[0][:], b[0][:], 0.0, high[0][:], MIN, MAX)
+        cap(1)
+        nc.vector.tensor_tensor(median[:, 0:CHUNK], low[0][:], a[0][:], ADD)
+        nc.sync.dma_start(out[:, 0:CHUNK], median[:, 0:CHUNK])
+        finish(1)
+        bounds(2)
+        bounds(3)
+        cap(2)
+        cap(3)
+        finish(2)
+        finish(3)

@@ -128,59 +128,55 @@ def tile_picked_median_gelu_p_kernel(
                 multiply(1, codes1, g)
                 nc.scalar.activation(y[:, g * GROUP : (g + 1) * GROUP], banks[g][:], GELU)
 
-        def neighbours(d, j):
-            return y[:].indirect(pos_sb[d][:, j * CHUNK // STRIPE : (j + 1) * CHUNK // STRIPE])
+        def neighbours(d, begin, end):
+            return y[:].indirect(pos_sb[d][:, begin // STRIPE : end // STRIPE])
 
-        def square(name):
-            return keep.tile([P, CHUNK], F32, name=name, tag=name, align_bytes=64)
+        def values(name, width):
+            return keep.tile([P, width], F32, name=name, tag=name, align_bytes=64)
 
-        chunks = V // CHUNK
-        a = [square(f"a{j}") for j in range(chunks)]
-        b = [square(f"b{j}") for j in range(chunks)]
-        c = [square(f"c{j}") for j in range(chunks)]
-        high = [square(f"high{j}") for j in range(chunks)]
-        low = [square(f"low{j}") for j in range(chunks)]
-        capped = [square(f"capped{j}") for j in range(chunks)]
+        fused = CHUNK
+        wide = slice(0, 2 * CHUNK)
+        late = slice(2 * CHUNK, 3 * CHUNK)
+        a_fused = values("a_fused", fused)
+        d1 = values("d1", fused)
+        d2 = values("d2", fused)
+        cut = values("cut", fused)
+        shift = values("shift", fused)
+        plain = V - fused
+        a = values("a", plain)
+        b_wide = values("b_wide", 2 * CHUNK)
+        b_late = values("b_late", CHUNK)
+        c = values("c", plain)
+        high = values("high", plain)
+        low = values("low", plain)
+        capped = values("capped", plain)
         median = keep.tile([P, V], F32, name="median", align_bytes=256)
+        squares = [slice(j * CHUNK, (j + 1) * CHUNK) for j in range(plain // CHUNK)]
 
-        def fetch(tile, d, j):
-            nc.scalar.activation(tile[j][:], neighbours(d, j), COPY)
+        def fetch(tile, d, s):
+            nc.scalar.activation(tile, neighbours(d, fused + s.start, fused + s.stop), COPY)
 
-        def bounds(j):
-            nc.vector.tensor_tensor(high[j][:], a[j][:], b[j][:], MAX)
-            nc.vector.tensor_tensor(low[j][:], a[j][:], b[j][:], MIN)
+        nc.scalar.activation(a_fused[:], neighbours(0, 0, fused), COPY)
+        fetch(a[:, wide], 0, wide)
+        fetch(a[:, late], 0, late)
+        fetch(b_late[:], 1, late)
+        for s in squares:
+            fetch(c[:, s], 2, s)
 
-        def cap(j):
-            nc.vector.tensor_tensor(capped[j][:], high[j][:], c[j][:], MIN)
-
-        def finish(j):
-            columns = slice(j * CHUNK, (j + 1) * CHUNK)
-            nc.vector.tensor_tensor(median[:, columns], low[j][:], capped[j][:], MAX)
+        nc.vector.tensor_copy(b_wide[:], neighbours(1, fused + wide.start, fused + wide.stop))
+        nc.vector.tensor_tensor(d1[:], neighbours(1, 0, fused), a_fused[:], SUB)
+        nc.vector.tensor_tensor(d2[:], neighbours(2, 0, fused), a_fused[:], SUB)
+        nc.vector.tensor_tensor(high[:, wide], a[:, wide], b_wide[:], MAX)
+        nc.vector.scalar_tensor_tensor(cut[:], d1[:], 0.0, d2[:], MAX, MIN)
+        nc.vector.tensor_tensor(low[:, wide], a[:, wide], b_wide[:], MIN)
+        nc.vector.scalar_tensor_tensor(shift[:], d1[:], 0.0, cut[:], MIN, MAX)
+        nc.vector.tensor_tensor(high[:, late], a[:, late], b_late[:], MAX)
+        nc.vector.tensor_tensor(low[:, late], a[:, late], b_late[:], MIN)
+        nc.vector.tensor_tensor(median[:, 0:fused], shift[:], a_fused[:], ADD)
+        nc.sync.dma_start(out[:, 0:fused], median[:, 0:fused])
+        for s in squares:
+            nc.vector.tensor_tensor(capped[:, s], high[:, s], c[:, s], MIN)
+        for s in squares:
+            columns = slice(fused + s.start, fused + s.stop)
+            nc.vector.tensor_tensor(median[:, columns], low[:, s], capped[:, s], MAX)
             nc.sync.dma_start(out[:, columns], median[:, columns])
-
-        fetch(a, 0, 0)
-        fetch(a, 0, 1)
-        fetch(c, 2, 1)
-        for j in (2, 3):
-            fetch(a, 0, j)
-            fetch(b, 1, j)
-        for j in (2, 3):
-            fetch(c, 2, j)
-
-        nc.vector.tensor_copy(b[1][:], neighbours(1, 1))
-        nc.vector.tensor_tensor(b[0][:], neighbours(1, 0), a[0][:], SUB)
-        nc.vector.tensor_tensor(c[0][:], neighbours(2, 0), a[0][:], SUB)
-        nc.vector.tensor_tensor(high[1][:], a[1][:], b[1][:], MAX)
-        nc.vector.scalar_tensor_tensor(high[0][:], b[0][:], 0.0, c[0][:], MAX, MIN)
-        nc.vector.tensor_tensor(low[1][:], a[1][:], b[1][:], MIN)
-        nc.vector.scalar_tensor_tensor(low[0][:], b[0][:], 0.0, high[0][:], MIN, MAX)
-        cap(1)
-        nc.vector.tensor_tensor(median[:, 0:CHUNK], low[0][:], a[0][:], ADD)
-        nc.sync.dma_start(out[:, 0:CHUNK], median[:, 0:CHUNK])
-        finish(1)
-        bounds(2)
-        bounds(3)
-        cap(2)
-        cap(3)
-        finish(2)
-        finish(3)

@@ -128,55 +128,54 @@ def tile_picked_median_gelu_p_kernel(
                 multiply(1, codes1, g)
                 nc.scalar.activation(y[:, g * GROUP : (g + 1) * GROUP], banks[g][:], GELU)
 
-        def neighbours(d, begin, end):
-            return y[:].indirect(pos_sb[d][:, begin // STRIPE : end // STRIPE])
+        def neighbours(d, targets):
+            return y[:].indirect(pos_sb[d][:, targets.start // STRIPE : targets.stop // STRIPE])
 
-        def values(name, width):
-            return keep.tile([P, width], F32, name=name, tag=name, align_bytes=64)
+        def values(name):
+            return keep.tile([P, V], F32, name=name, tag=name, align_bytes=256)
 
-        fused = CHUNK
-        wide = slice(0, 2 * CHUNK)
-        late = slice(2 * CHUNK, 3 * CHUNK)
-        a_fused = values("a_fused", fused)
-        d1 = values("d1", fused)
-        d2 = values("d2", fused)
-        cut = values("cut", fused)
-        shift = values("shift", fused)
-        plain = V - fused
-        a = values("a", plain)
-        b_wide = values("b_wide", 2 * CHUNK)
-        b_late = values("b_late", CHUNK)
-        c = values("c", plain)
-        high = values("high", plain)
-        low = values("low", plain)
-        capped = values("capped", plain)
-        median = keep.tile([P, V], F32, name="median", align_bytes=256)
-        squares = [slice(j * CHUNK, (j + 1) * CHUNK) for j in range(plain // CHUNK)]
+        a, b, c, high, low, capped, median = [
+            values(name) for name in ("a", "b", "c", "high", "low", "capped", "median")
+        ]
+        fused, first, second, third = [slice(j * CHUNK, (j + 1) * CHUNK) for j in range(V // CHUNK)]
+        early = slice(first.start, second.stop)
+        halves = [slice(third.start + j * CHUNK // 2, third.start + (j + 1) * CHUNK // 2) for j in range(2)]
 
-        def fetch(tile, d, s):
-            nc.scalar.activation(tile, neighbours(d, fused + s.start, fused + s.stop), COPY)
+        for tile, d, targets in (
+            (a, 0, fused),
+            (a, 0, early),
+            (c, 2, early),
+            (a, 0, third),
+            (b, 1, third),
+            (c, 2, third),
+        ):
+            nc.scalar.activation(tile[:, targets], neighbours(d, targets), COPY)
 
-        nc.scalar.activation(a_fused[:], neighbours(0, 0, fused), COPY)
-        fetch(a[:, wide], 0, wide)
-        fetch(a[:, late], 0, late)
-        fetch(b_late[:], 1, late)
-        for s in squares:
-            fetch(c[:, s], 2, s)
+        def step(result, left, right, op, targets):
+            nc.vector.tensor_tensor(result[:, targets], left[:, targets], right[:, targets], op)
 
-        nc.vector.tensor_copy(b_wide[:], neighbours(1, fused + wide.start, fused + wide.stop))
-        nc.vector.tensor_tensor(d1[:], neighbours(1, 0, fused), a_fused[:], SUB)
-        nc.vector.tensor_tensor(d2[:], neighbours(2, 0, fused), a_fused[:], SUB)
-        nc.vector.tensor_tensor(high[:, wide], a[:, wide], b_wide[:], MAX)
-        nc.vector.scalar_tensor_tensor(cut[:], d1[:], 0.0, d2[:], MAX, MIN)
-        nc.vector.tensor_tensor(low[:, wide], a[:, wide], b_wide[:], MIN)
-        nc.vector.scalar_tensor_tensor(shift[:], d1[:], 0.0, cut[:], MIN, MAX)
-        nc.vector.tensor_tensor(high[:, late], a[:, late], b_late[:], MAX)
-        nc.vector.tensor_tensor(low[:, late], a[:, late], b_late[:], MIN)
-        nc.vector.tensor_tensor(median[:, 0:fused], shift[:], a_fused[:], ADD)
-        nc.sync.dma_start(out[:, 0:fused], median[:, 0:fused])
-        for s in squares:
-            nc.vector.tensor_tensor(capped[:, s], high[:, s], c[:, s], MIN)
-        for s in squares:
-            columns = slice(fused + s.start, fused + s.stop)
-            nc.vector.tensor_tensor(median[:, columns], low[:, s], capped[:, s], MAX)
-            nc.sync.dma_start(out[:, columns], median[:, columns])
+        def store(targets):
+            nc.sync.dma_start(out[:, targets], median[:, targets])
+
+        nc.vector.tensor_copy(b[:, early], neighbours(1, early))
+        nc.vector.tensor_tensor(b[:, fused], neighbours(1, fused), a[:, fused], SUB)
+        nc.vector.tensor_tensor(c[:, fused], neighbours(2, fused), a[:, fused], SUB)
+        step(high, a, b, MAX, early)
+        nc.vector.scalar_tensor_tensor(capped[:, fused], b[:, fused], 0.0, c[:, fused], MAX, MIN)
+        step(low, a, b, MIN, early)
+        nc.vector.scalar_tensor_tensor(low[:, fused], b[:, fused], 0.0, capped[:, fused], MIN, MAX)
+        step(capped, high, c, MIN, first)
+        step(capped, high, c, MIN, second)
+        step(median, low, a, ADD, fused)
+        store(fused)
+        step(high, a, b, MAX, third)
+        step(median, low, capped, MAX, first)
+        store(first)
+        step(low, a, b, MIN, third)
+        for half in halves:
+            step(capped, high, c, MIN, half)
+        step(median, low, capped, MAX, second)
+        store(second)
+        for half in halves:
+            step(median, low, capped, MAX, half)
+        store(third)

@@ -30,7 +30,7 @@ STRIPE = 16
 RUN = 4
 GROUP = 128
 PIECES = (384, 384, 256)
-CHUNK = 128
+QUARTER = V // 4
 GAP_TO_LISTS = 48 * 1024
 GAP_TO_OTHERS = 64 * 1024
 
@@ -51,7 +51,7 @@ def tile_picked_median_gelu_p_kernel(
         scale_table = tables.tile([P, T], U8, name="scale_table", align_bytes=256)
         nc.sync.dma_start(
             scale_table[first_row:P, :].bitcast(I32),
-            x_scales.rearrange("z q c -> (z q) c").bitcast(I32),
+            x_scales.rearrange("z q c -> q z c").bitcast(I32),
         )
         offs_sb = lists.tile([P, S // STRIPE], U16, name="offs_sb")
         nc.sync.dma_start(offs_sb[:], offs)
@@ -72,19 +72,19 @@ def tile_picked_median_gelu_p_kernel(
         nc.sync.dma_start(word_table[1][:].bitcast(I32), x_words[1].bitcast(I32))
 
         w_bf = first_gap.tile([P, PASSES, M, PACK], BF16, name="w_bf", align_bytes=64, offset=GAP_TO_LISTS)
+
         x_planes = second_gap.tile([P, PASSES * S], U8, name="x_planes", align_bytes=64, offset=GAP_TO_OTHERS)
         nc.vector.memset(x_planes[:].bitcast(I32), 0)
         x_plane = [x_planes[:, z * S : (z + 1) * S] for z in range(PASSES)]
 
         picked_scales = keep.tile([P, S], U8, name="picked_scales", align_bytes=64)
         nc.vector.tensor_copy(picked_scales[:], scale_table[:].indirect(offs_sb[:]))
-        for z in range(PASSES):
-            for q in range(P // QUADRANT):
-                row = first_row + SCALE_ROWS * z + QUADRANT_ROWS * q
-                nc.sync.dma_start(
-                    x_plane[z][QUADRANT * q : QUADRANT * q + QUADRANT_ROWS, :].bitcast(I32),
-                    picked_scales[row : row + QUADRANT_ROWS, :].bitcast(I32),
-                )
+        for q in range(P // QUADRANT):
+            row = first_row + PASSES * QUADRANT_ROWS * q
+            nc.sync.dma_start(
+                x_planes[QUADRANT * q : QUADRANT * q + QUADRANT_ROWS, :].bitcast(I32),
+                picked_scales[row : row + PASSES * QUADRANT_ROWS, :].bitcast(I32),
+            )
 
         banks = [psum.tile([M, GROUP], F32, name=f"bank{g}", tag=f"bank{g}") for g in range(S // GROUP)]
         y = tables.tile([P, S], F32, name="y", align_bytes=256)
@@ -131,15 +131,13 @@ def tile_picked_median_gelu_p_kernel(
         def neighbours(d, targets):
             return y[:].indirect(pos_sb[d][:, targets.start // STRIPE : targets.stop // STRIPE])
 
-        def values(name):
-            return keep.tile([P, V], F32, name=name, tag=name, align_bytes=256)
-
         a, b, c, high, low, capped, median = [
-            values(name) for name in ("a", "b", "c", "high", "low", "capped", "median")
+            keep.tile([P, V], F32, name=name, tag=name, align_bytes=256)
+            for name in ("a", "b", "c", "high", "low", "capped", "median")
         ]
-        fused, first, second, third = [slice(j * CHUNK, (j + 1) * CHUNK) for j in range(V // CHUNK)]
+        fused, first, second, third = [slice(j * QUARTER, (j + 1) * QUARTER) for j in range(V // QUARTER)]
         early = slice(first.start, second.stop)
-        halves = [slice(third.start + j * CHUNK // 2, third.start + (j + 1) * CHUNK // 2) for j in range(2)]
+        halves = [slice(third.start + j * QUARTER // 2, third.start + (j + 1) * QUARTER // 2) for j in range(2)]
 
         for tile, d, targets in (
             (a, 0, fused),

@@ -165,10 +165,9 @@ def tile_picked_median_gelu_p_kernel(
         step(capped, high, c, MIN, first)
         step(capped, high, c, MIN, second)
         step(median, low, a, ADD, fused)
-        store(fused)
         step(high, a, b, MAX, third)
         step(median, low, capped, MAX, first)
-        store(first)
+        store(slice(fused.start, first.stop))
         step(low, a, b, MIN, third)
         for half in halves:
             step(capped, high, c, MIN, half)

@@ -33,6 +33,9 @@ PIECES = (384, 384, 256)
 QUARTER = V // 4
 GAP_TO_LISTS = 48 * 1024
 GAP_TO_OTHERS = 64 * 1024
+GAP_TO_FETCHED = 32 * 1024
+GAP_TO_LATE = 64 * 1024
+GAP_TO_C = 24 * 1024
 
 
 def tile_picked_median_gelu_p_kernel(
@@ -45,6 +48,7 @@ def tile_picked_median_gelu_p_kernel(
         lists = ctx.enter_context(tc.tile_pool(name="lists", bufs=1))
         second_gap = ctx.enter_context(tc.tile_pool(name="second_gap", bufs=1))
         keep = ctx.enter_context(tc.tile_pool(name="keep", bufs=1))
+        fetched = ctx.enter_context(tc.tile_pool(name="fetched", bufs=1))
         psum = ctx.enter_context(tc.psum_pool(name="psum", bufs=1))
 
         first_row = P - PASSES * SCALE_ROWS
@@ -131,10 +135,16 @@ def tile_picked_median_gelu_p_kernel(
         def neighbours(d, targets):
             return y[:].indirect(pos_sb[d][:, targets.start // STRIPE : targets.stop // STRIPE])
 
-        a, b, c, high, low, capped, median = [
+        b, difference, high, low, capped, median = [
             keep.tile([P, V], F32, name=name, tag=name, align_bytes=256)
-            for name in ("a", "b", "c", "high", "low", "capped", "median")
+            for name in ("b", "difference", "high", "low", "capped", "median")
         ]
+        a = fetched.tile([P, V], F32, name="a", align_bytes=256, offset=GAP_TO_FETCHED)
+        late_a, late_b = [
+            fetched.tile([P, V], F32, name=name, align_bytes=256, offset=GAP_TO_LATE + j * V * 4)
+            for j, name in enumerate(("late_a", "late_b"))
+        ]
+        c = second_gap.tile([P, V], F32, name="c", align_bytes=256, offset=GAP_TO_C)
         fused, first, second, third = [slice(j * QUARTER, (j + 1) * QUARTER) for j in range(V // QUARTER)]
         early = slice(first.start, second.stop)
         halves = [slice(third.start + j * QUARTER // 2, third.start + (j + 1) * QUARTER // 2) for j in range(2)]
@@ -142,10 +152,9 @@ def tile_picked_median_gelu_p_kernel(
         for tile, d, targets in (
             (a, 0, fused),
             (a, 0, early),
-            (c, 2, early),
-            (a, 0, third),
-            (b, 1, third),
-            (c, 2, third),
+            (c, 2, slice(early.start, V)),
+            (late_a, 0, third),
+            (late_b, 1, third),
         ):
             nc.scalar.activation(tile[:, targets], neighbours(d, targets), COPY)
 
@@ -157,20 +166,19 @@ def tile_picked_median_gelu_p_kernel(
 
         nc.vector.tensor_copy(b[:, early], neighbours(1, early))
         nc.vector.tensor_tensor(b[:, fused], neighbours(1, fused), a[:, fused], SUB)
-        nc.vector.tensor_tensor(c[:, fused], neighbours(2, fused), a[:, fused], SUB)
+        nc.vector.tensor_tensor(difference[:, fused], neighbours(2, fused), a[:, fused], SUB)
         step(high, a, b, MAX, early)
-        nc.vector.scalar_tensor_tensor(capped[:, fused], b[:, fused], 0.0, c[:, fused], MAX, MIN)
+        nc.vector.scalar_tensor_tensor(capped[:, fused], b[:, fused], 0.0, difference[:, fused], MAX, MIN)
         step(low, a, b, MIN, early)
         nc.vector.scalar_tensor_tensor(low[:, fused], b[:, fused], 0.0, capped[:, fused], MIN, MAX)
-        step(capped, high, c, MIN, first)
-        step(capped, high, c, MIN, second)
+        step(capped, high, c, MIN, early)
+        step(high, late_a, c, MAX, third)
         step(median, low, a, ADD, fused)
-        step(high, a, b, MAX, third)
         step(median, low, capped, MAX, first)
         store(slice(fused.start, first.stop))
-        step(low, a, b, MIN, third)
+        step(low, late_a, c, MIN, third)
         for half in halves:
-            step(capped, high, c, MIN, half)
+            step(capped, high, late_b, MIN, half)
         step(median, low, capped, MAX, second)
         store(second)
         for half in halves:

from contextlib import ExitStack

import concourse.mybir as mybir

K, T, S, V, M = 1024, 2048, 1024, 512, 128
FLOPS = 2 * K * M * S

F32 = mybir.dt.float32
BF16 = mybir.dt.bfloat16
I32 = mybir.dt.int32
U32 = mybir.dt.uint32
U16 = mybir.dt.uint16
U8 = mybir.dt.uint8
FP8X4 = mybir.dt.float8_e4m3fn_x4
FP4X4 = mybir.dt.float4_e2m1fn_x4
MAX = mybir.AluOpType.max
MIN = mybir.AluOpType.min
ADD = mybir.AluOpType.add
SUB = mybir.AluOpType.subtract
COPY = mybir.ActivationFunctionType.Copy
GELU = mybir.ActivationFunctionType.Gelu_apprx_tanh

P = 128
PACK = 4
PASSES = K // (P * PACK)
SCALE_ROWS = 16
QUADRANT = 32
QUADRANT_ROWS = SCALE_ROWS * QUADRANT // P
STRIPE = 16
RUN = 4
GROUP = 128
PIECES = (384, 384, 256)
QUARTER = V // 4
GAP_TO_LISTS = 48 * 1024
GAP_TO_OTHERS = 64 * 1024
GAP_TO_FETCHED = 32 * 1024
GAP_TO_LATE = 64 * 1024
GAP_TO_C = 24 * 1024


def tile_picked_median_gelu_p_kernel(
    tc, x_words, x_scales, w1, offs, pos1, pos2, pos3, out
):
    nc = tc.nc
    with ExitStack() as ctx:
        tables = ctx.enter_context(tc.tile_pool(name="tables", bufs=1))
        first_gap = ctx.enter_context(tc.tile_pool(name="first_gap", bufs=1))
        lists = ctx.enter_context(tc.tile_pool(name="lists", bufs=1))
        second_gap = ctx.enter_context(tc.tile_pool(name="second_gap", bufs=1))
        keep = ctx.enter_context(tc.tile_pool(name="keep", bufs=1))
        fetched = ctx.enter_context(tc.tile_pool(name="fetched", bufs=1))
        psum = ctx.enter_context(tc.psum_pool(name="psum", bufs=1))

        first_row = P - PASSES * SCALE_ROWS
        scale_table = tables.tile([P, T], U8, name="scale_table", align_bytes=256)
        nc.sync.dma_start(
            scale_table[first_row:P, :].bitcast(I32),
            x_scales.rearrange("z q c -> q z c").bitcast(I32),
        )
        offs_sb = lists.tile([P, S // STRIPE], U16, name="offs_sb")
        nc.sync.dma_start(offs_sb[:], offs)
        nc.vector.memset(scale_table[0:first_row, :].bitcast(I32), 0)

        word_table = [
            tables.tile([P, width], U16, name=f"word_table{z}", align_bytes=256) for z, width in enumerate((2 * T, T))
        ]
        w_raw = [keep.tile([P, PACK, M], F32, name=f"w_raw{z}", tag=f"w_raw{z}", align_bytes=64) for z in range(PASSES)]
        pos_sb = []
        for d, pos in enumerate((pos1, pos2, pos3)):
            pos_tile = lists.tile([P, V // STRIPE], U16, name=f"pos_sb{d}")
            nc.sync.dma_start(pos_tile[:], pos)
            pos_sb.append(pos_tile)
        nc.sync.dma_start(word_table[0][:, :T].bitcast(I32), x_words[0].bitcast(I32))
        for z in range(PASSES):
            nc.sync.dma_start(w_raw[z][:], w1.rearrange("(z p j) m -> z p j m", z=PASSES, j=PACK)[z])
        nc.sync.dma_start(word_table[1][:].bitcast(I32), x_words[1].bitcast(I32))

        w_bf = first_gap.tile([P, PASSES, M, PACK], BF16, name="w_bf", align_bytes=64, offset=GAP_TO_LISTS)

        x_planes = second_gap.tile([P, PASSES * S], U8, name="x_planes", align_bytes=64, offset=GAP_TO_OTHERS)
        nc.vector.memset(x_planes[:].bitcast(I32), 0)
        x_plane = [x_planes[:, z * S : (z + 1) * S] for z in range(PASSES)]

        picked_scales = keep.tile([P, S], U8, name="picked_scales", align_bytes=64)
        nc.vector.tensor_copy(picked_scales[:], scale_table[:].indirect(offs_sb[:]))
        for q in range(P // QUADRANT):
            row = first_row + PASSES * QUADRANT_ROWS * q
            nc.sync.dma_start(
                x_planes[QUADRANT * q : QUADRANT * q + QUADRANT_ROWS, :].bitcast(I32),
                picked_scales[row : row + PASSES * QUADRANT_ROWS, :].bitcast(I32),
            )

        banks = [psum.tile([M, GROUP], F32, name=f"bank{g}", tag=f"bank{g}") for g in range(S // GROUP)]
        y = tables.tile([P, S], F32, name="y", align_bytes=256)

        codes0 = keep.tile([P, S], U16, name="codes0", align_bytes=64)
        nc.vector.tensor_copy(codes0[:], word_table[0][:].indirect(offs_sb[:]))

        for z in range(PASSES):
            nc.scalar.copy(
                w_bf[:, z].rearrange("p (c i) j -> p c j i", i=RUN),
                w_raw[z][:].rearrange("p j (c i) -> p c j i", i=RUN),
            )
        w_codes = keep.tile([P, PASSES * M], U32, name="w_codes", align_bytes=64)
        w_plane = keep.tile([P, PASSES * M], U8, name="w_plane", align_bytes=64)
        nc.vector.quantize_mx(
            out=w_codes[:].bitcast(FP8X4), scales=w_plane[:], in_=w_bf[:].rearrange("p z m j -> p (z m j)")
        )

        def multiply(z, codes, g):
            columns = slice(g * GROUP, (g + 1) * GROUP)
            nc.tensor.matmul_mx(
                out=banks[g][:],
                lhsT=w_codes[:, z * M : (z + 1) * M].bitcast(FP8X4),
                lhsT_scale=w_plane[:, z * M : (z + 1) * M],
                rhs=codes[:, columns].bitcast(FP4X4),
                rhs_scale=x_plane[z][:, columns],
                start=(z == 0),
                stop=(z == PASSES - 1),
            )

        codes1 = keep.tile([P, S], U16, name="codes1", tag="w_raw1", align_bytes=64)
        for g in range(S // GROUP):
            multiply(0, codes0, g)
        for i, width in enumerate(PIECES):
            begin = sum(PIECES[:i])
            end = begin + width
            nc.vector.tensor_copy(
                codes1[:, begin:end], word_table[1][:].indirect(offs_sb[:, begin // STRIPE : end // STRIPE])
            )
            for g in range(begin // GROUP, end // GROUP):
                multiply(1, codes1, g)
                nc.scalar.activation(y[:, g * GROUP : (g + 1) * GROUP], banks[g][:], GELU)

        def neighbours(d, targets):
            return y[:].indirect(pos_sb[d][:, targets.start // STRIPE : targets.stop // STRIPE])

        b, difference, high, low, capped, median = [
            keep.tile([P, V], F32, name=name, tag=name, align_bytes=256)
            for name in ("b", "difference", "high", "low", "capped", "median")
        ]
        a = fetched.tile([P, V], F32, name="a", align_bytes=256, offset=GAP_TO_FETCHED)
        late_a, late_b = [
            fetched.tile([P, V], F32, name=name, align_bytes=256, offset=GAP_TO_LATE + j * V * 4)
            for j, name in enumerate(("late_a", "late_b"))
        ]
        c = second_gap.tile([P, V], F32, name="c", align_bytes=256, offset=GAP_TO_C)
        fused, first, second, third = [slice(j * QUARTER, (j + 1) * QUARTER) for j in range(V // QUARTER)]
        early = slice(first.start, second.stop)
        halves = [slice(third.start + j * QUARTER // 2, third.start + (j + 1) * QUARTER // 2) for j in range(2)]

        for tile, d, targets in (
            (a, 0, fused),
            (a, 0, early),
            (c, 2, slice(early.start, V)),
            (late_a, 0, third),
            (late_b, 1, third),
        ):
            nc.scalar.activation(tile[:, targets], neighbours(d, targets), COPY)

        def step(result, left, right, op, targets):
            nc.vector.tensor_tensor(result[:, targets], left[:, targets], right[:, targets], op)

        def store(targets):
            nc.sync.dma_start(out[:, targets], median[:, targets])

        nc.vector.tensor_copy(b[:, early], neighbours(1, early))
        nc.vector.tensor_tensor(b[:, fused], neighbours(1, fused), a[:, fused], SUB)
        nc.vector.tensor_tensor(difference[:, fused], neighbours(2, fused), a[:, fused], SUB)
        step(high, a, b, MAX, early)
        nc.vector.scalar_tensor_tensor(capped[:, fused], b[:, fused], 0.0, difference[:, fused], MAX, MIN)
        step(low, a, b, MIN, early)
        nc.vector.scalar_tensor_tensor(low[:, fused], b[:, fused], 0.0, capped[:, fused], MIN, MAX)
        step(capped, high, c, MIN, early)
        step(high, late_a, c, MAX, third)
        step(median, low, a, ADD, fused)
        step(median, low, capped, MAX, first)
        store(slice(fused.start, first.stop))
        step(low, late_a, c, MIN, third)
        for half in halves:
            step(capped, high, late_b, MIN, half)
        step(median, low, capped, MAX, second)
        store(second)
        for half in halves:
            step(median, low, capped, MAX, half)
        store(third)
